import numpy as np
import ml_dtypes


def mxq(x, axis, fmt="e4m3"):
    dtype, down = {"e4m3": (ml_dtypes.float8_e4m3fn, 7), "e5m2": (ml_dtypes.float8_e5m2, 14)}[fmt]
    v = np.moveaxis(np.asarray(x, np.float32).astype(ml_dtypes.bfloat16).astype(np.float64), axis, -1)
    blocks = v.reshape(v.shape[:-1] + (-1, 32))
    amax = np.abs(blocks).max(-1, keepdims=True)
    byte = np.maximum(np.where(amax > 0, np.frexp(amax)[1] - 1 + 127, 0) - down, 1)
    scale = np.exp2(byte - 127.0)
    codes = (blocks / scale).astype(np.float32).astype(dtype).astype(np.float64)
    return np.moveaxis((codes * scale).reshape(v.shape), -1, axis)


WIDE = False


def mx_kscale(k):
    if not WIDE:
        return np.ones(k)
    levels = np.array([10, -10, 5, -5, 0])
    if k % 512:
        return np.exp2(np.random.permutation(np.resize(levels, k // 32))).repeat(32)
    a = np.empty((k // 512, 16))
    for p in range(k // 512):
        a[p, :8] = np.random.permutation(np.resize(levels, 8))
        for g in range(8):
            far = levels[np.abs(levels - a[p, g]) >= 10]
            a[p, g + 8] = far[np.random.randint(len(far))]
    return np.exp2(a.ravel()).repeat(32)


BF16 = ml_dtypes.bfloat16


def bf(x):
    return np.asarray(x, np.float32).astype(BF16)


def f64(x):
    return np.asarray(x).astype(np.float64)


E2M1 = np.array([0.0, 0.5, 1.0, 1.5, 2.0, 3.0, 4.0, 6.0, -0.0, -0.5, -1.0, -1.5, -2.0, -3.0, -4.0, -6.0])


def pack_weight(w, fmt):
    k, n = w.shape
    w = f64(bf(w)).reshape(k // 32, 32, n)
    amax = np.abs(w).max(1)
    if fmt == "e4m3":
        byte = np.frexp(amax)[1] - 1 + 127 - 7
    else:
        mant, ex = np.frexp(amax / 6.0)
        byte = np.where(mant > 0.5, ex, ex - 1) + 127
    byte = np.clip(np.where(amax > 0, byte, 1), 1, 254)
    scaled = (w * np.exp2(127.0 - byte)[:, None, :]).reshape(k, n).astype(np.float32)
    by_word = np.ascontiguousarray(scaled.reshape(k // 512, 128, 4, n).transpose(0, 1, 3, 2))
    if fmt == "e4m3":
        words = by_word.astype(ml_dtypes.float8_e4m3fn).view(np.uint8)
    else:
        c = by_word.astype(ml_dtypes.float4_e2m1fn).view(np.uint8) & 0xF
        words = c[..., 0::2] | (c[..., 1::2] << 4)
    return np.ascontiguousarray(words), np.ascontiguousarray(byte.astype(np.uint8).reshape(k // 512, 16, n))


def unpack_weight(words, scales, fmt):
    g, p, n, _ = words.shape
    if fmt == "e4m3":
        vals = np.ascontiguousarray(words).view(ml_dtypes.float8_e4m3fn).astype(np.float64)
    else:
        nib = np.empty((g, p, n, 4), np.uint8)
        nib[..., 0::2] = words & 0xF
        nib[..., 1::2] = words >> 4
        vals = E2M1[nib]
    vals = vals * np.repeat(np.exp2(scales.astype(np.float64) - 127.0), 8, axis=1)[..., None]
    return vals.transpose(0, 1, 3, 2).reshape(g * 512, n)
def pack4(w):
    words, scales = pack_weight(w, "e2m1")
    return words.reshape(words.shape[0], 128, -1), scales


def unpack4(words, scales):
    return unpack_weight(words.reshape(words.shape[0], 128, -1, 2), scales, "e2m1")


def planes(Y):
    n, m = Y.shape
    b = f64(bf(Y)).reshape(n // 32, 32, m)
    amax = np.abs(b).max(1)
    byte = np.clip(np.where(amax > 0, np.frexp(amax)[1] - 1 + 127 - 7, 1), 1, 254)
    codes = (b * np.exp2(127.0 - byte)[:, None, :]).reshape(n, m).astype(np.float32).astype(ml_dtypes.float8_e4m3fn).view(np.uint8)
    words = codes.reshape(n // 512, 128, 4, m).transpose(0, 1, 3, 2)
    return np.ascontiguousarray(words), np.ascontiguousarray(byte.astype(np.uint8).reshape(n // 512, 16, m))


S, F, C = 2048, 1024, 1024

def setup_inputs():
    s = mx_kscale(F)
    t = mx_kscale(S)
    x = np.random.laplace(0.0, np.sqrt(0.5), (S, F))
    w = np.random.randn(F, C) / np.sqrt(F)
    x_words, x_scales = pack_weight((x * s[None, :]).T, "e4m3")
    w_words, w_scales = pack4(w / s[:, None])
    return {
        "x_words": x_words, "x_scales": x_scales,
        "w_words": w_words, "w_scales": w_scales,
        "x_rows": bf(x / t[:, None]),
        "sample_weight": bf(np.exp(0.3 * np.random.randn(S)) * t),
        "gain": bf(np.sqrt(F) * np.exp(0.8 * np.random.randn(C))),
    }

def reference(x_words, x_scales, w_words, w_scales, x_rows, sample_weight, gain):
    X = unpack_weight(x_words, x_scales, "e4m3")
    W = unpack4(w_words, w_scales)
    z = X.T @ W
    h = f64(sample_weight)[:, None] * np.tanh(z)
    rq = mxq(f64(x_rows), 0, "e4m3")
    hq = mxq(h, 0, "e4m3")
    moment = rq.T @ hq
    y = moment / S * f64(gain)[None, :]
    Y = y.T
    words, scales = planes(Y)
    return y, words, scales

@@ -1,0 +1,236 @@
+from contextlib import ExitStack
+
+import concourse.mybir as mybir
+from concourse.masks import make_identity
+
+S, F, C = 2048, 1024, 1024
+FLOPS = 2 * S * F * C * 2
+
+F32 = mybir.dt.float32
+BF16 = mybir.dt.bfloat16
+I32 = mybir.dt.int32
+U8 = mybir.dt.uint8
+FP8X4 = mybir.dt.float8_e4m3fn_x4
+FP4X4 = mybir.dt.float4_e2m1fn_x4
+ACT = mybir.ActivationFunctionType
+ALU = mybir.AluOpType
+
+P = 128
+NSG = 4
+NFT = 8
+ZB, AB, TB, RB = 3, 3, 2, 3
+WSTORE = [(0, 2), (2, 4), (4, 6), (6, 7), (7, 8)]
+
+PLAN = [('xperm', 0), ('xsperm', 0), ('mm1', 0, 0), ('mm1', 0, 1), ('tanh', 0, 0), ('tanh', 0, 1), ('xperm', 1), ('xsperm', 1), ('wmul', 0), ('mm1', 1, 0), ('mm1', 1, 1), ('tanh', 1, 0), ('tanh', 1, 1), ('wmul', 1), ('qh', 0), ('mm1', 2, 0), ('mm1', 2, 1), ('tanh', 2, 0), ('tanh', 2, 1), ('xperm', 2), ('xsperm', 2), ('wmul', 2), ('qh', 1), ('mm1', 3, 0), ('mm1', 3, 1), ('tanh', 3, 0), ('tanh', 3, 1), ('wmul', 3), ('qh', 2), ('rintA', 0, 0), ('mm1', 4, 0), ('mm1', 4, 1), ('tanh', 4, 0), ('tanh', 4, 1), ('xperm', 3), ('xsperm', 3), ('wmul', 4), ('qh', 3), ('mm1', 5, 0), ('mm1', 5, 1), ('tanh', 5, 0), ('tanh', 5, 1), ('wmul', 5), ('qh', 4), ('rintA', 1, 0), ('mm1', 6, 0), ('mm1', 6, 1), ('tanh', 6, 0), ('tanh', 6, 1), ('wmul', 6), ('qh', 5), ('mm1', 7, 0), ('mm1', 7, 1), ('tanh', 7, 0), ('tanh', 7, 1), ('wmul', 7), ('qh', 6), ('rintA', 0, 1), ('mm1', 8, 0), ('mm1', 8, 1), ('tanh', 8, 0), ('tanh', 8, 1), ('wmul', 8), ('qh', 7), ('rintA', 1, 1), ('mm1', 9, 0), ('mm1', 9, 1), ('tanh', 9, 0), ('tanh', 9, 1), ('wmul', 9), ('qh', 8), ('mm1', 10, 0), ('mm1', 10, 1), ('tanh', 10, 0), ('tanh', 10, 1), ('wmul', 10), ('qh', 9), ('rintA', 0, 2), ('mm1', 11, 0), ('mm1', 11, 1), ('tanh', 11, 0), ('tanh', 11, 1), ('wmul', 11), ('qh', 10), ('rintA', 1, 2), ('mm1', 12, 0), ('mm1', 12, 1), ('tanh', 12, 0), ('tanh', 12, 1), ('wmul', 12), ('qh', 11), ('mm1', 13, 0), ('mm1', 13, 1), ('tanh', 13, 0), ('tanh', 13, 1), ('wmul', 13), ('qh', 12), ('rintA', 0, 3), ('mm1', 14, 0), ('mm1', 14, 1), ('tanh', 14, 0), ('tanh', 14, 1), ('wmul', 14), ('qh', 13), ('rintA', 1, 3), ('qr', 0), ('mm1', 15, 0), ('mm1', 15, 1), ('tanh', 15, 0), ('tanh', 15, 1), ('wmul', 15), ('qh', 14), ('qr', 1), ('qh', 15), ('mm2', 0, 0), ('gain', 0, 0), ('cast', 0, 0), ('rintA', 2, 3), ('rintV', 2, 0), ('rintV', 2, 1), ('rintV', 2, 2), ('mm2', 0, 1), ('gain', 0, 1), ('cast', 0, 1), ('qr', 2), ('mm2', 1, 0), ('gain', 1, 0), ('cast', 1, 0), ('rintA', 3, 3), ('rintV', 3, 0), ('rintV', 3, 1), ('rintV', 3, 2), ('mm2', 1, 1), ('tr', (0, 0), (0, 1)), ('gain', 1, 1), ('trcopy', (0, 0), (0, 1)), ('cast', 1, 1), ('qr', 3), ('mm2', 2, 0), ('gain', 2, 0), ('qy', 0, 0), ('qy', 0, 1), ('cast', 2, 0), ('rintA', 4, 3), ('rintV', 4, 0), ('rintV', 4, 1), ('rintV', 4, 2), ('mm2', 2, 1), ('tr', (1, 0), (1, 1)), ('gain', 2, 1), ('trcopy', (1, 0), (1, 1)), ('cast', 2, 1), ('qr', 4), ('mm2', 3, 0), ('gain', 3, 0), ('qy', 1, 0), ('qy', 1, 1), ('cast', 3, 0), ('rintA', 5, 3), ('rintV', 5, 0), ('rintV', 5, 1), ('rintV', 5, 2), ('mm2', 3, 1), ('tr', (2, 0), (2, 1)), ('gain', 3, 1), ('trcopy', (2, 0), (2, 1)), ('cast', 3, 1), ('qr', 5), ('mm2', 4, 0), ('gain', 4, 0), ('qy', 2, 0), ('qy', 2, 1), ('cast', 4, 0), ('rintA', 6, 3), ('rintV', 6, 0), ('rintV', 6, 1), ('rintV', 6, 2), ('mm2', 4, 1), ('tr', (3, 0), (3, 1)), ('gain', 4, 1), ('trcopy', (3, 0), (3, 1)), ('cast', 4, 1), ('qr', 6), ('mm2', 5, 0), ('gain', 5, 0), ('qy', 3, 0), ('qy', 3, 1), ('cast', 5, 0), ('rintA', 7, 3), ('rintV', 7, 0), ('rintV', 7, 1), ('rintV', 7, 2), ('mm2', 5, 1), ('tr', (4, 0), (4, 1)), ('gain', 5, 1), ('trcopy', (4, 0), (4, 1)), ('cast', 5, 1), ('qr', 7), ('mm2', 6, 0), ('gain', 6, 0), ('qy', 4, 0), ('qy', 4, 1), ('cast', 6, 0), ('mm2', 6, 1), ('tr', (5, 0), (5, 1)), ('gain', 6, 1), ('trcopy', (5, 0), (5, 1)), ('cast', 6, 1), ('mm2', 7, 0), ('gain', 7, 0), ('qy', 5, 0), ('qy', 5, 1), ('cast', 7, 0), ('mm2', 7, 1), ('tr', (6, 0), (6, 1)), ('gain', 7, 1), ('trcopy', (6, 0), (6, 1)), ('cast', 7, 1), ('qy', 6, 0), ('qy', 6, 1), ('tr', (7, 0), (7, 1)), ('trcopy', (7, 0), (7, 1)), ('qy', 7, 0), ('qy', 7, 1)]
+
+
+def tile_tanh_cross_moment_planes_h2_kernel(
+    tc, x_words, x_scales, w_words, w_scales, x_rows, sample_weight, gain, out_0, out_1, out_2
+):
+    nc = tc.nc
+    with ExitStack() as ctx:
+        keep = ctx.enter_context(tc.tile_pool(name="keep", bufs=1))
+        work = ctx.enter_context(tc.tile_pool(name="work", bufs=3))
+        psum = ctx.enter_context(tc.psum_pool(name="psum", bufs=1))
+        ctx.enter_context(tc.manual_schedule())
+
+        x_raw = keep.tile([P, NSG, 2, 512], I32, align_bytes=64)
+        xs_raw = keep.tile([P, 2, 512], I32, align_bytes=64)
+        x_codes = keep.tile([P, NSG, 4, 2, P], I32, align_bytes=64)
+        x_scl = keep.tile([P, NSG, 4, 2, 32], I32, align_bytes=64)
+        w_codes = keep.tile([P, 2, 512], I32, align_bytes=64)
+        w_scl = keep.tile([P, 2, 256], I32, align_bytes=64)
+        r_raw = keep.tile([P, NSG, 4, F], BF16, align_bytes=64)
+        sw_raw = keep.tile([P, NSG, 16], BF16, align_bytes=64)
+        sw = keep.tile([P, NSG, 4], F32, align_bytes=64)
+        gain_all = keep.tile([P, C], BF16, align_bytes=64)
+        ident = keep.tile([P, P], F32, align_bytes=64)
+        warm = keep.tile([P, 8], F32, align_bytes=64)
+        h_codes = keep.tile([P, NSG, C], I32, align_bytes=64)
+        h_scl = keep.tile([P, NSG, C], U8, align_bytes=64)
+        r_codes = keep.tile([P, NFT, NSG, P], I32, align_bytes=64)
+        r_scl = keep.tile([P, NFT, NSG, P], U8, align_bytes=64)
+        y_codes = keep.tile([P, 2, F], I32, align_bytes=64)
+        y_scl = keep.tile([P, 2, F], U8, align_bytes=64)
+
+        xw = x_words.rearrange("g p n t -> p g (n t)").bitcast(I32)
+        ww = w_words.rearrange("g p b -> p g b").bitcast(I32)
+        xs = x_scales.rearrange("g q n -> q g n").bitcast(I32)
+        ws = w_scales.rearrange("g q n -> q g n").bitcast(I32)
+        swv = sample_weight.rearrange("(s j k) -> j s k", s=NSG, k=16)
+        o1 = out_1.rearrange("g p m t -> p g (m t)").bitcast(I32)
+        o2 = out_2.rearrange("g q n -> q g n").bitcast(I32)
+
+        nc.vector.memset(warm[:], 0.0)
+        nc.vector.memset(w_scl[:], 0)
+        nc.vector.memset(xs_raw[:], 0)
+        nc.sync.dma_start(out=x_raw[:, 0], in_=xw[:, :, 0:512])
+        nc.sync.dma_start(out=w_codes[:], in_=ww)
+        for q in range(4):
+            eng = nc.sync if q < 2 else nc.gpsimd
+            eng.dma_start(out=w_scl[32 * q : 32 * q + 4], in_=ws[4 * q : 4 * q + 4])
+        nc.scalar.activation(out=warm[:, 4:8], in_=warm[:, 0:4], func=ACT.Tanh)
+        for q in range(4):
+            nc.scalar.dma_start(out=xs_raw[32 * q : 32 * q + 4], in_=xs[4 * q : 4 * q + 4])
+        nc.sync.dma_start(out=x_raw[:, 1], in_=xw[:, :, 512:1024])
+        for r in range(4):
+            nc.sync.dma_start(out=sw_raw[r:P:4, :, 0:13], in_=swv[:, :, r : r + 13])
+        for sg in range(2, NSG):
+            nc.sync.dma_start(out=x_raw[:, sg], in_=xw[:, :, 512 * sg : 512 * (sg + 1)])
+        for sg in range(NSG):
+            rows = x_rows[512 * sg : 512 * (sg + 1), :].rearrange("(j t r) f -> r j t f", t=4, r=4)
+            for r in range(4):
+                nc.sync.dma_start(out=r_raw[r:P:4, sg], in_=rows[r])
+        nc.sync.dma_start(out=gain_all[:], in_=gain.partition_broadcast(P))
+        make_identity(nc, ident[:])
+
+        z_bank, t_tile, h_tile, r_tile, acc_bank, y_tile, yb_tile, tr_bank, yw_of = {}, {}, {}, {}, {}, {}, {}, {}, {}
+        count = {"z": 0, "acc": 0, "tr": 0}
+
+        def xperm(sg):
+            nc.vector.tensor_copy(
+                out=x_codes[:, sg].rearrange("p t g (j r) -> p t (g j) r", r=4),
+                in_=x_raw[:, sg].rearrange("p g (j t r) -> p t (g j) r", t=4, r=4),
+            )
+
+        def xsperm(sg):
+            nc.vector.tensor_copy(
+                out=x_scl[:, sg],
+                in_=xs_raw[:, :, 128 * sg : 128 * (sg + 1)].rearrange("p g (j t) -> p t g j", t=4),
+            )
+
+        def mm1(k, h):
+            sg, c0 = (k // 2) % 4, 512 * (k // 8) + 256 * (k % 2) + 128 * h
+            bank = psum.tile([P, 4, P], F32, name="z%d" % (count["z"] % ZB))
+            count["z"] += 1
+            z_bank[k, h] = bank
+            for t in range(4):
+                for g in range(2):
+                    nc.tensor.matmul_mx(
+                        out=bank[:, t, :],
+                        lhsT=x_codes[:, sg, t, g, :].bitcast(FP8X4),
+                        lhsT_scale=x_scl[:, sg, t, g, :].bitcast(U8),
+                        rhs=w_codes[:, g, c0 // 2 : c0 // 2 + 64].bitcast(U8).bitcast(FP4X4),
+                        rhs_scale=w_scl[:, g, c0 // 4 : c0 // 4 + 32].bitcast(U8),
+                        start=(g == 0),
+                        stop=(g == 1),
+                    )
+
+        def tanh(k, h):
+            if h == 0:
+                t_tile[k] = work.tile([P, 256, 4], F32, name="tanh_z", align_bytes=64)
+            nc.scalar.activation(
+                out=t_tile[k][:, 128 * h : 128 * (h + 1), :],
+                in_=z_bank[k, h][:].rearrange("p t n -> p n t"),
+                func=ACT.Tanh,
+            )
+
+        def wmul(k):
+            sg = (k // 2) % 4
+            if k == 0:
+                nc.vector.tensor_copy(out=sw[:], in_=sw_raw[:, :, 0:13:4])
+            h_tile[k] = work.tile([P, 256, 4], BF16, name="h_bf", align_bytes=64)
+            nc.vector.tensor_tensor(
+                out=h_tile[k][:],
+                in0=t_tile[k][:],
+                in1=sw[:, sg, :].unsqueeze(1).to_broadcast([P, 256, 4]),
+                op=ALU.mult,
+            )
+
+        def qh(k):
+            sg, c0 = (k // 2) % 4, 512 * (k // 8) + 256 * (k % 2)
+            nc.vector.quantize_mx(
+                out=h_codes[:, sg, c0 : c0 + 256].bitcast(FP8X4),
+                scales=h_scl[:, sg, c0 : c0 + 256],
+                in_=h_tile[k][:].rearrange("p n t -> p (n t)"),
+            )
+
+        def rint(ft, sg, copy):
+            if ft not in r_tile:
+                r_tile[ft] = work.tile([P, NSG, P, 4], BF16, name="r_bf", align_bytes=64, bufs=RB)
+            copy(
+                out=r_tile[ft][:, sg].rearrange("p (c i) t -> p c t i", i=4),
+                in_=r_raw[:, sg, :, P * ft : P * (ft + 1)].rearrange("p t (c i) -> p c t i", i=4),
+            )
+
+        def qr(ft):
+            nc.vector.quantize_mx(
+                out=r_codes[:, ft].rearrange("p s f -> p (s f)").bitcast(FP8X4),
+                scales=r_scl[:, ft].rearrange("p s f -> p (s f)"),
+                in_=r_tile[ft][:].rearrange("p s f t -> p (s f t)"),
+            )
+
+        def mm2(ft, ch):
+            bank = psum.tile([P, 512], F32, name="acc%d" % (count["acc"] % AB))
+            count["acc"] += 1
+            acc_bank[ft, ch] = bank
+            for sg in range(NSG):
+                nc.tensor.matmul_mx(
+                    out=bank[:],
+                    lhsT=r_codes[:, ft, sg, :].bitcast(FP8X4),
+                    lhsT_scale=r_scl[:, ft, sg, :],
+                    rhs=h_codes[:, sg, 512 * ch : 512 * (ch + 1)].bitcast(FP8X4),
+                    rhs_scale=h_scl[:, sg, 512 * ch : 512 * (ch + 1)],
+                    start=(sg == 0),
+                    stop=(sg == NSG - 1),
+                )
+
+        def scale_out(ft, ch):
+            y = work.tile([P, 512], F32, name="y", bufs=4, align_bytes=64)
+            y_tile[ft, ch] = y
+            nc.vector.scalar_tensor_tensor(
+                out=y[:],
+                in0=acc_bank[ft, ch][:],
+                scalar=1.0 / S,
+                in1=gain_all[:, 512 * ch : 512 * (ch + 1)],
+                op0=ALU.mult,
+                op1=ALU.mult,
+            )
+            nc.sync.dma_start(out=out_0[P * ft : P * (ft + 1), 512 * ch : 512 * (ch + 1)], in_=y[:])
+
+        def cast(ft, ch):
+            yb = work.tile([P, 2, P, 2], BF16, name="y_bf", bufs=4, align_bytes=64)
+            yb_tile[ft, ch] = yb
+            nc.scalar.copy(out=yb[:], in_=y_tile[ft, ch][:].rearrange("p (q u e) -> p u q e", u=2, e=2))
+
+        def tr(*units):
+            bank = psum.tile([P, 2, 2, P], F32, name="tr%d" % (count["tr"] % TB))
+            count["tr"] += 1
+            tr_bank[units] = bank
+            for i, unit in enumerate(units):
+                words = yb_tile[unit][:].rearrange("p u q e -> p u (q e)").bitcast(F32)
+                for u in range(2):
+                    nc.tensor.transpose(bank[:, i, u, :], words[:, u, :], ident[:])
+
+        def trcopy(*units):
+            n = len(units)
+            yw = work.tile([P, 2, P, 2], F32, name="y_words", align_bytes=64)
+            nc.scalar.copy(out=yw[:, :n], in_=tr_bank[units][:, :n].rearrange("p i u f -> p i f u"))
+            for i, unit in enumerate(units):
+                yw_of[unit] = yw[:, i].rearrange("p f u -> p (f u)").bitcast(BF16)
+
+        done_y = set()
+
+        def qy(ft, ch):
+            nc.vector.quantize_mx(
+                out=y_codes[:, ch, P * ft : P * (ft + 1)].bitcast(FP8X4),
+                scales=y_scl[:, ch, P * ft : P * (ft + 1)],
+                in_=yw_of[ft, ch],
+            )
+            done_y.add((ft, ch))
+            for lo, hi in WSTORE:
+                if lo <= ft < hi and all((f, c) in done_y for f in range(lo, hi) for c in range(2)):
+                    nc.sync.dma_start(out=o1[:, :, P * lo : P * hi], in_=y_codes[:, :, P * lo : P * hi])
+            if len(done_y) == 2 * NFT:
+                for q in range(4):
+                    eng = nc.sync if q % 2 == 0 else nc.scalar
+                    eng.dma_start(out=o2[4 * q : 4 * q + 4], in_=y_scl[32 * q : 32 * q + 4].bitcast(I32))
+
+        steps = {
+            "xperm": xperm, "xsperm": xsperm, "mm1": mm1, "tanh": tanh, "wmul": wmul, "qh": qh,
+            "rintA": lambda ft, sg: rint(ft, sg, nc.scalar.copy),
+            "rintV": lambda ft, sg: rint(ft, sg, nc.vector.tensor_copy),
+            "qr": qr, "mm2": mm2, "gain": scale_out, "cast": cast, "tr": tr, "trcopy": trcopy, "qy": qy,
+        }
+        for step in PLAN:
+            steps[step[0]](*step[1:])

@@ -18,10 +18,10 @@ ALU = mybir.AluOpType
 P = 128
 NSG = 4
 NFT = 8
-ZB, AB, TB, RB = 3, 3, 2, 3
+AB, RB = 5, 8
 WSTORE = [(0, 2), (2, 4), (4, 6), (6, 7), (7, 8)]
 
-PLAN = [('xperm', 0), ('xsperm', 0), ('mm1', 0, 0), ('mm1', 0, 1), ('tanh', 0, 0), ('tanh', 0, 1), ('xperm', 1), ('xsperm', 1), ('wmul', 0), ('mm1', 1, 0), ('mm1', 1, 1), ('tanh', 1, 0), ('tanh', 1, 1), ('wmul', 1), ('qh', 0), ('mm1', 2, 0), ('mm1', 2, 1), ('tanh', 2, 0), ('tanh', 2, 1), ('xperm', 2), ('xsperm', 2), ('wmul', 2), ('qh', 1), ('mm1', 3, 0), ('mm1', 3, 1), ('tanh', 3, 0), ('tanh', 3, 1), ('wmul', 3), ('qh', 2), ('rintA', 0, 0), ('mm1', 4, 0), ('mm1', 4, 1), ('tanh', 4, 0), ('tanh', 4, 1), ('xperm', 3), ('xsperm', 3), ('wmul', 4), ('qh', 3), ('mm1', 5, 0), ('mm1', 5, 1), ('tanh', 5, 0), ('tanh', 5, 1), ('wmul', 5), ('qh', 4), ('rintA', 1, 0), ('mm1', 6, 0), ('mm1', 6, 1), ('tanh', 6, 0), ('tanh', 6, 1), ('wmul', 6), ('qh', 5), ('mm1', 7, 0), ('mm1', 7, 1), ('tanh', 7, 0), ('tanh', 7, 1), ('wmul', 7), ('qh', 6), ('rintA', 0, 1), ('mm1', 8, 0), ('mm1', 8, 1), ('tanh', 8, 0), ('tanh', 8, 1), ('wmul', 8), ('qh', 7), ('rintA', 1, 1), ('mm1', 9, 0), ('mm1', 9, 1), ('tanh', 9, 0), ('tanh', 9, 1), ('wmul', 9), ('qh', 8), ('mm1', 10, 0), ('mm1', 10, 1), ('tanh', 10, 0), ('tanh', 10, 1), ('wmul', 10), ('qh', 9), ('rintA', 0, 2), ('mm1', 11, 0), ('mm1', 11, 1), ('tanh', 11, 0), ('tanh', 11, 1), ('wmul', 11), ('qh', 10), ('rintA', 1, 2), ('mm1', 12, 0), ('mm1', 12, 1), ('tanh', 12, 0), ('tanh', 12, 1), ('wmul', 12), ('qh', 11), ('mm1', 13, 0), ('mm1', 13, 1), ('tanh', 13, 0), ('tanh', 13, 1), ('wmul', 13), ('qh', 12), ('rintA', 0, 3), ('mm1', 14, 0), ('mm1', 14, 1), ('tanh', 14, 0), ('tanh', 14, 1), ('wmul', 14), ('qh', 13), ('rintA', 1, 3), ('qr', 0), ('mm1', 15, 0), ('mm1', 15, 1), ('tanh', 15, 0), ('tanh', 15, 1), ('wmul', 15), ('qh', 14), ('qr', 1), ('qh', 15), ('mm2', 0, 0), ('gain', 0, 0), ('cast', 0, 0), ('rintA', 2, 3), ('rintV', 2, 0), ('rintV', 2, 1), ('rintV', 2, 2), ('mm2', 0, 1), ('gain', 0, 1), ('cast', 0, 1), ('qr', 2), ('mm2', 1, 0), ('gain', 1, 0), ('cast', 1, 0), ('rintA', 3, 3), ('rintV', 3, 0), ('rintV', 3, 1), ('rintV', 3, 2), ('mm2', 1, 1), ('tr', (0, 0), (0, 1)), ('gain', 1, 1), ('trcopy', (0, 0), (0, 1)), ('cast', 1, 1), ('qr', 3), ('mm2', 2, 0), ('gain', 2, 0), ('qy', 0, 0), ('qy', 0, 1), ('cast', 2, 0), ('rintA', 4, 3), ('rintV', 4, 0), ('rintV', 4, 1), ('rintV', 4, 2), ('mm2', 2, 1), ('tr', (1, 0), (1, 1)), ('gain', 2, 1), ('trcopy', (1, 0), (1, 1)), ('cast', 2, 1), ('qr', 4), ('mm2', 3, 0), ('gain', 3, 0), ('qy', 1, 0), ('qy', 1, 1), ('cast', 3, 0), ('rintA', 5, 3), ('rintV', 5, 0), ('rintV', 5, 1), ('rintV', 5, 2), ('mm2', 3, 1), ('tr', (2, 0), (2, 1)), ('gain', 3, 1), ('trcopy', (2, 0), (2, 1)), ('cast', 3, 1), ('qr', 5), ('mm2', 4, 0), ('gain', 4, 0), ('qy', 2, 0), ('qy', 2, 1), ('cast', 4, 0), ('rintA', 6, 3), ('rintV', 6, 0), ('rintV', 6, 1), ('rintV', 6, 2), ('mm2', 4, 1), ('tr', (3, 0), (3, 1)), ('gain', 4, 1), ('trcopy', (3, 0), (3, 1)), ('cast', 4, 1), ('qr', 6), ('mm2', 5, 0), ('gain', 5, 0), ('qy', 3, 0), ('qy', 3, 1), ('cast', 5, 0), ('rintA', 7, 3), ('rintV', 7, 0), ('rintV', 7, 1), ('rintV', 7, 2), ('mm2', 5, 1), ('tr', (4, 0), (4, 1)), ('gain', 5, 1), ('trcopy', (4, 0), (4, 1)), ('cast', 5, 1), ('qr', 7), ('mm2', 6, 0), ('gain', 6, 0), ('qy', 4, 0), ('qy', 4, 1), ('cast', 6, 0), ('mm2', 6, 1), ('tr', (5, 0), (5, 1)), ('gain', 6, 1), ('trcopy', (5, 0), (5, 1)), ('cast', 6, 1), ('mm2', 7, 0), ('gain', 7, 0), ('qy', 5, 0), ('qy', 5, 1), ('cast', 7, 0), ('mm2', 7, 1), ('tr', (6, 0), (6, 1)), ('gain', 7, 1), ('trcopy', (6, 0), (6, 1)), ('cast', 7, 1), ('qy', 6, 0), ('qy', 6, 1), ('tr', (7, 0), (7, 1)), ('trcopy', (7, 0), (7, 1)), ('qy', 7, 0), ('qy', 7, 1)]
+PLAN = [('xperm', 0), ('xsperm', 0), ('mm1', 0, 0), ('mm1', 0, 1), ('swperm',), ('xperm', 1), ('xsperm', 1), ('xperm', 2), ('xsperm', 2), ('tanh', 0, 0), ('tanh', 0, 1), ('swturn',), ('mm1', 1, 0), ('mm1', 1, 1), ('xperm', 3), ('xsperm', 3), ('wmul', 0), ('tanh', 1, 0), ('tanh', 1, 1), ('mm1', 2, 0), ('mm1', 2, 1), ('wmul', 1), ('tanh', 2, 0), ('tanh', 2, 1), ('qh', 0), ('mm1', 3, 0), ('mm1', 3, 1), ('wmul', 2), ('tanh', 3, 0), ('tanh', 3, 1), ('qh', 1), ('mm1', 4, 0), ('mm1', 4, 1), ('wmul', 3), ('tanh', 4, 0), ('tanh', 4, 1), ('qh', 2), ('mm1', 5, 0), ('mm1', 5, 1), ('wmul', 4), ('tanh', 5, 0), ('tanh', 5, 1), ('qh', 3), ('mm1', 6, 0), ('mm1', 6, 1), ('wmul', 5), ('tanh', 6, 0), ('tanh', 6, 1), ('qh', 4), ('mm1', 7, 0), ('mm1', 7, 1), ('wmul', 6), ('tanh', 7, 0), ('tanh', 7, 1), ('qh', 5), ('mm1', 8, 0), ('mm1', 8, 1), ('rintA', 0, 1), ('wmul', 7), ('tanh', 8, 0), ('tanh', 8, 1), ('qh', 6), ('mm1', 9, 0), ('mm1', 9, 1), ('wmul', 8), ('tanh', 9, 0), ('tanh', 9, 1), ('qh', 7), ('mm1', 10, 0), ('mm1', 10, 1), ('wmul', 9), ('tanh', 10, 0), ('tanh', 10, 1), ('qh', 8), ('mm1', 11, 0), ('mm1', 11, 1), ('wmul', 10), ('tanh', 11, 0), ('tanh', 11, 1), ('qh', 9), ('mm1', 12, 0), ('mm1', 12, 1), ('wmul', 11), ('tanh', 12, 0), ('tanh', 12, 1), ('qh', 10), ('mm1', 13, 0), ('mm1', 13, 1), ('wmul', 12), ('tanh', 13, 0), ('tanh', 13, 1), ('qh', 11), ('rintA', 0, 2), ('rintA', 0, 3), ('mm1', 14, 0), ('rintV', 0, 0), ('mm1', 14, 1), ('wmul', 13), ('qr', 0, 0, 1, 2, 3), ('tanh', 14, 0), ('tanh', 14, 1), ('qh', 12), ('rintA', 1, 1), ('rintA', 1, 2), ('rintA', 1, 3), ('mm1', 15, 0), ('rintV', 1, 0), ('mm1', 15, 1), ('wmul', 14), ('qr', 1, 0, 1, 2, 3), ('tanh', 15, 0), ('tanh', 15, 1), ('qh', 13), ('mm2', 0, 0), ('wmul', 15), ('qh', 14), ('mm2', 1, 0), ('qh', 15), ('gain', 0, 0), ('rintA', 2, 2), ('rintA', 2, 3), ('mm2', 0, 1), ('rintV', 2, 0), ('rintV', 2, 1), ('qr', 2, 0, 1, 2, 3), ('gain', 1, 0), ('mm2', 1, 1), ('cast', 0, 0), ('gain', 0, 1), ('rintA', 3, 1), ('rintA', 3, 2), ('rintA', 3, 3), ('mm2', 2, 0), ('rintV', 3, 0), ('qr', 3, 0, 1, 2, 3), ('cast', 1, 0), ('gain', 1, 1), ('mm2', 2, 1), ('cast', 0, 1), ('gain', 2, 0), ('rintA', 4, 0), ('rintA', 4, 1), ('rintA', 4, 2), ('rintA', 4, 3), ('mm2', 3, 0), ('qr', 4, 0, 1, 2, 3), ('cast', 1, 1), ('gain', 2, 1), ('mm2', 3, 1), ('tr', (0, 0), (1, 0)), ('tr', (0, 1), (1, 1)), ('cast', 2, 0), ('gain', 3, 0), ('rintA', 5, 1), ('rintA', 5, 2), ('rintA', 5, 3), ('mm2', 4, 0), ('rintV', 5, 0), ('qr', 5, 0, 1, 2, 3), ('cast', 2, 1), ('gain', 3, 1), ('mm2', 4, 1), ('trcopy', (0, 0), (1, 0)), ('trcopy', (0, 1), (1, 1)), ('cast', 3, 0), ('gain', 4, 0), ('mm2', 5, 0), ('rintV', 6, 0), ('rintV', 6, 1), ('rintV', 6, 2), ('rintV', 6, 3), ('qr', 6, 0, 1, 2, 3), ('cast', 3, 1), ('gain', 4, 1), ('mm2', 5, 1), ('qy', 0, 0), ('qy', 1, 0), ('qy', 0, 1), ('qy', 1, 1), ('tr', (2, 0), (2, 1)), ('tr', (3, 0), (3, 1)), ('cast', 4, 0), ('gain', 5, 0), ('rintA', 7, 1), ('rintA', 7, 2), ('rintA', 7, 3), ('mm2', 6, 0), ('rintV', 7, 0), ('qr', 7, 0, 1, 2, 3), ('cast', 4, 1), ('gain', 5, 1), ('mm2', 6, 1), ('trcopy', (2, 0), (2, 1)), ('trcopy', (3, 0), (3, 1)), ('cast', 5, 0), ('gain', 6, 0), ('mm2', 7, 0), ('cast', 5, 1), ('gain', 6, 1), ('mm2', 7, 1), ('qy', 2, 0), ('qy', 2, 1), ('qy', 3, 0), ('qy', 3, 1), ('tr', (4, 0), (4, 1)), ('tr', (5, 0), (5, 1)), ('cast', 6, 0), ('gain', 7, 0), ('castV', 6, 1), ('gain', 7, 1), ('trcopy', (4, 0), (4, 1)), ('trcopy', (5, 0), (5, 1)), ('tr', (6, 0), (6, 1)), ('castV', 7, 0), ('castV', 7, 1), ('trcopy', (6, 0), (6, 1)), ('qy', 4, 0), ('qy', 4, 1), ('qy', 5, 0), ('qy', 5, 1), ('tr', (7, 0), (7, 1)), ('trcopy', (7, 0), (7, 1)), ('qy', 6, 0), ('qy', 6, 1), ('qy', 7, 0), ('qy', 7, 1)]
 
 
 def tile_tanh_cross_moment_planes_h2_kernel(
@@ -35,13 +35,15 @@ def tile_tanh_cross_moment_planes_h2_kernel(
         ctx.enter_context(tc.manual_schedule())
 
         x_raw = keep.tile([P, NSG, 2, 512], I32, align_bytes=64)
-        xs_raw = keep.tile([P, 2, 512], I32, align_bytes=64)
+        xs_first = keep.tile([P, 2, 128], I32, align_bytes=64)
+        xs_rest = keep.tile([P, 2, 384], I32, align_bytes=64)
         x_codes = keep.tile([P, NSG, 4, 2, P], I32, align_bytes=64)
         x_scl = keep.tile([P, NSG, 4, 2, 32], I32, align_bytes=64)
         w_codes = keep.tile([P, 2, 512], I32, align_bytes=64)
         w_scl = keep.tile([P, 2, 256], I32, align_bytes=64)
         r_raw = keep.tile([P, NSG, 4, F], BF16, align_bytes=64)
-        sw_raw = keep.tile([P, NSG, 16], BF16, align_bytes=64)
+        sw_raw = keep.tile([NSG, 512], BF16, align_bytes=64)
+        sw_rows = keep.tile([P, 4, P], F32, align_bytes=64)
         sw = keep.tile([P, NSG, 4], F32, align_bytes=64)
         gain_all = keep.tile([P, C], BF16, align_bytes=64)
         ident = keep.tile([P, P], F32, align_bytes=64)
@@ -57,24 +59,26 @@ def tile_tanh_cross_moment_planes_h2_kernel(
         ww = w_words.rearrange("g p b -> p g b").bitcast(I32)
         xs = x_scales.rearrange("g q n -> q g n").bitcast(I32)
         ws = w_scales.rearrange("g q n -> q g n").bitcast(I32)
-        swv = sample_weight.rearrange("(s j k) -> j s k", s=NSG, k=16)
         o1 = out_1.rearrange("g p m t -> p g (m t)").bitcast(I32)
         o2 = out_2.rearrange("g q n -> q g n").bitcast(I32)
 
-        nc.vector.memset(warm[:], 0.0)
+        nc.vector.memset(xs_first[:], 0)
         nc.vector.memset(w_scl[:], 0)
-        nc.vector.memset(xs_raw[:], 0)
+        nc.vector.memset(warm[:], 0.0)
+        nc.vector.memset(xs_rest[:], 0)
+        nc.vector.memset(sw_rows[:], 0.0)
         nc.sync.dma_start(out=x_raw[:, 0], in_=xw[:, :, 0:512])
-        nc.sync.dma_start(out=w_codes[:], in_=ww)
+        nc.scalar.dma_start(out=w_codes[:], in_=ww)
         for q in range(4):
-            eng = nc.sync if q < 2 else nc.gpsimd
+            nc.sync.dma_start(out=xs_first[32 * q : 32 * q + 4], in_=xs[4 * q : 4 * q + 4, :, 0:128])
+        for q in range(4):
+            eng = nc.scalar if q < 2 else nc.sync
             eng.dma_start(out=w_scl[32 * q : 32 * q + 4], in_=ws[4 * q : 4 * q + 4])
         nc.scalar.activation(out=warm[:, 4:8], in_=warm[:, 0:4], func=ACT.Tanh)
-        for q in range(4):
-            nc.scalar.dma_start(out=xs_raw[32 * q : 32 * q + 4], in_=xs[4 * q : 4 * q + 4])
+        nc.sync.dma_start(out=sw_raw[:], in_=sample_weight.rearrange("(s n) -> s n", s=NSG))
         nc.sync.dma_start(out=x_raw[:, 1], in_=xw[:, :, 512:1024])
-        for r in range(4):
-            nc.sync.dma_start(out=sw_raw[r:P:4, :, 0:13], in_=swv[:, :, r : r + 13])
+        for q in range(4):
+            nc.sync.dma_start(out=xs_rest[32 * q : 32 * q + 4], in_=xs[4 * q : 4 * q + 4, :, 128:512])
         for sg in range(2, NSG):
             nc.sync.dma_start(out=x_raw[:, sg], in_=xw[:, :, 512 * sg : 512 * (sg + 1)])
         for sg in range(NSG):
@@ -96,12 +100,24 @@ def tile_tanh_cross_moment_planes_h2_kernel(
         def xsperm(sg):
             nc.vector.tensor_copy(
                 out=x_scl[:, sg],
-                in_=xs_raw[:, :, 128 * sg : 128 * (sg + 1)].rearrange("p g (j t) -> p t g j", t=4),
+                in_=(xs_first[:] if sg == 0 else xs_rest[:, :, 128 * (sg - 1) : 128 * sg]).rearrange("p g (j t) -> p t g j", t=4),
             )
+
+        def swperm():
+            nc.vector.tensor_copy(
+                out=sw_rows[0:NSG].rearrange("s t (j r) -> s t j r", r=4),
+                in_=sw_raw[:].rearrange("s (j t r) -> s t j r", t=4, r=4),
+            )
+
+        def swturn():
+            bank = psum.tile([P, 4, P], F32, name="bank7")
+            for t in range(4):
+                nc.tensor.transpose(bank[:, t, :], sw_rows[:, t, :], ident[:])
+            nc.scalar.copy(out=sw[:], in_=bank[:, :, 0:NSG].rearrange("p t s -> p s t"))
 
         def mm1(k, h):
             sg, c0 = (k // 2) % 4, 512 * (k // 8) + 256 * (k % 2) + 128 * h
-            bank = psum.tile([P, 4, P], F32, name="z%d" % (count["z"] % ZB))
+            bank = psum.tile([P, 4, P], F32, name="bank%d" % (count["z"] % 3))
             count["z"] += 1
             z_bank[k, h] = bank
             for t in range(4):
@@ -118,7 +134,7 @@ def tile_tanh_cross_moment_planes_h2_kernel(
 
         def tanh(k, h):
             if h == 0:
-                t_tile[k] = work.tile([P, 256, 4], F32, name="tanh_z", align_bytes=64)
+                t_tile[k] = work.tile([P, 256, 4], F32, name="tanh_z", bufs=5, align_bytes=64)
             nc.scalar.activation(
                 out=t_tile[k][:, 128 * h : 128 * (h + 1), :],
                 in_=z_bank[k, h][:].rearrange("p t n -> p n t"),
@@ -127,8 +143,6 @@ def tile_tanh_cross_moment_planes_h2_kernel(
 
         def wmul(k):
             sg = (k // 2) % 4
-            if k == 0:
-                nc.vector.tensor_copy(out=sw[:], in_=sw_raw[:, :, 0:13:4])
             h_tile[k] = work.tile([P, 256, 4], BF16, name="h_bf", align_bytes=64)
             nc.vector.tensor_tensor(
                 out=h_tile[k][:],
@@ -153,7 +167,7 @@ def tile_tanh_cross_moment_planes_h2_kernel(
                 in_=r_raw[:, sg, :, P * ft : P * (ft + 1)].rearrange("p t (c i) -> p c t i", i=4),
             )
 
-        def qr(ft):
+        def qr(ft, *unused):
             nc.vector.quantize_mx(
                 out=r_codes[:, ft].rearrange("p s f -> p (s f)").bitcast(FP8X4),
                 scales=r_scl[:, ft].rearrange("p s f -> p (s f)"),
@@ -161,7 +175,7 @@ def tile_tanh_cross_moment_planes_h2_kernel(
             )
 
         def mm2(ft, ch):
-            bank = psum.tile([P, 512], F32, name="acc%d" % (count["acc"] % AB))
+            bank = psum.tile([P, 512], F32, name="bank%d" % (3 + count["acc"] % AB))
             count["acc"] += 1
             acc_bank[ft, ch] = bank
             for sg in range(NSG):
@@ -176,7 +190,7 @@ def tile_tanh_cross_moment_planes_h2_kernel(
                 )
 
         def scale_out(ft, ch):
-            y = work.tile([P, 512], F32, name="y", bufs=4, align_bytes=64)
+            y = work.tile([P, 512], F32, name="y", bufs=6, align_bytes=64)
             y_tile[ft, ch] = y
             nc.vector.scalar_tensor_tensor(
                 out=y[:],
@@ -188,13 +202,13 @@ def tile_tanh_cross_moment_planes_h2_kernel(
             )
             nc.sync.dma_start(out=out_0[P * ft : P * (ft + 1), 512 * ch : 512 * (ch + 1)], in_=y[:])
 
-        def cast(ft, ch):
-            yb = work.tile([P, 2, P, 2], BF16, name="y_bf", bufs=4, align_bytes=64)
+        def cast(ft, ch, copy):
+            yb = work.tile([P, 2, P, 2], BF16, name="y_bf", bufs=6, align_bytes=64)
             yb_tile[ft, ch] = yb
-            nc.scalar.copy(out=yb[:], in_=y_tile[ft, ch][:].rearrange("p (q u e) -> p u q e", u=2, e=2))
+            copy(out=yb[:], in_=y_tile[ft, ch][:].rearrange("p (q u e) -> p u q e", u=2, e=2))
 
         def tr(*units):
-            bank = psum.tile([P, 2, 2, P], F32, name="tr%d" % (count["tr"] % TB))
+            bank = psum.tile([P, 2, 2, P], F32, name="bank%d" % (count["tr"] % 3))
             count["tr"] += 1
             tr_bank[units] = bank
             for i, unit in enumerate(units):
@@ -204,7 +218,7 @@ def tile_tanh_cross_moment_planes_h2_kernel(
 
         def trcopy(*units):
             n = len(units)
-            yw = work.tile([P, 2, P, 2], F32, name="y_words", align_bytes=64)
+            yw = work.tile([P, 2, P, 2], F32, name="y_words", bufs=4, align_bytes=64)
             nc.scalar.copy(out=yw[:, :n], in_=tr_bank[units][:, :n].rearrange("p i u f -> p i f u"))
             for i, unit in enumerate(units):
                 yw_of[unit] = yw[:, i].rearrange("p f u -> p (f u)").bitcast(BF16)
@@ -227,10 +241,10 @@ def tile_tanh_cross_moment_planes_h2_kernel(
                     eng.dma_start(out=o2[4 * q : 4 * q + 4], in_=y_scl[32 * q : 32 * q + 4].bitcast(I32))
 
         steps = {
-            "xperm": xperm, "xsperm": xsperm, "mm1": mm1, "tanh": tanh, "wmul": wmul, "qh": qh,
+            "swperm": swperm, "swturn": swturn, "xperm": xperm, "xsperm": xsperm, "mm1": mm1, "tanh": tanh, "wmul": wmul, "qh": qh,
             "rintA": lambda ft, sg: rint(ft, sg, nc.scalar.copy),
             "rintV": lambda ft, sg: rint(ft, sg, nc.vector.tensor_copy),
-            "qr": qr, "mm2": mm2, "gain": scale_out, "cast": cast, "tr": tr, "trcopy": trcopy, "qy": qy,
+            "qr": qr, "mm2": mm2, "gain": scale_out, "cast": lambda ft, ch: cast(ft, ch, nc.scalar.copy), "castV": lambda ft, ch: cast(ft, ch, nc.vector.tensor_copy), "tr": tr, "trcopy": trcopy, "qy": qy,
         }
         for step in PLAN:
             steps[step[0]](*step[1:])

@@ -18,10 +18,9 @@ ALU = mybir.AluOpType
 P = 128
 NSG = 4
 NFT = 8
-AB, RB = 5, 8
-WSTORE = [(0, 2), (2, 4), (4, 6), (6, 7), (7, 8)]
+RB = 8
 
-PLAN = [('xperm', 0), ('xsperm', 0), ('mm1', 0, 0), ('mm1', 0, 1), ('swperm',), ('xperm', 1), ('xsperm', 1), ('xperm', 2), ('xsperm', 2), ('tanh', 0, 0), ('tanh', 0, 1), ('swturn',), ('mm1', 1, 0), ('mm1', 1, 1), ('xperm', 3), ('xsperm', 3), ('wmul', 0), ('tanh', 1, 0), ('tanh', 1, 1), ('mm1', 2, 0), ('mm1', 2, 1), ('wmul', 1), ('tanh', 2, 0), ('tanh', 2, 1), ('qh', 0), ('mm1', 3, 0), ('mm1', 3, 1), ('wmul', 2), ('tanh', 3, 0), ('tanh', 3, 1), ('qh', 1), ('mm1', 4, 0), ('mm1', 4, 1), ('wmul', 3), ('tanh', 4, 0), ('tanh', 4, 1), ('qh', 2), ('mm1', 5, 0), ('mm1', 5, 1), ('wmul', 4), ('tanh', 5, 0), ('tanh', 5, 1), ('qh', 3), ('mm1', 6, 0), ('mm1', 6, 1), ('wmul', 5), ('tanh', 6, 0), ('tanh', 6, 1), ('qh', 4), ('mm1', 7, 0), ('mm1', 7, 1), ('wmul', 6), ('tanh', 7, 0), ('tanh', 7, 1), ('qh', 5), ('mm1', 8, 0), ('mm1', 8, 1), ('rintA', 0, 1), ('wmul', 7), ('tanh', 8, 0), ('tanh', 8, 1), ('qh', 6), ('mm1', 9, 0), ('mm1', 9, 1), ('wmul', 8), ('tanh', 9, 0), ('tanh', 9, 1), ('qh', 7), ('mm1', 10, 0), ('mm1', 10, 1), ('wmul', 9), ('tanh', 10, 0), ('tanh', 10, 1), ('qh', 8), ('mm1', 11, 0), ('mm1', 11, 1), ('wmul', 10), ('tanh', 11, 0), ('tanh', 11, 1), ('qh', 9), ('mm1', 12, 0), ('mm1', 12, 1), ('wmul', 11), ('tanh', 12, 0), ('tanh', 12, 1), ('qh', 10), ('mm1', 13, 0), ('mm1', 13, 1), ('wmul', 12), ('tanh', 13, 0), ('tanh', 13, 1), ('qh', 11), ('rintA', 0, 2), ('rintA', 0, 3), ('mm1', 14, 0), ('rintV', 0, 0), ('mm1', 14, 1), ('wmul', 13), ('qr', 0, 0, 1, 2, 3), ('tanh', 14, 0), ('tanh', 14, 1), ('qh', 12), ('rintA', 1, 1), ('rintA', 1, 2), ('rintA', 1, 3), ('mm1', 15, 0), ('rintV', 1, 0), ('mm1', 15, 1), ('wmul', 14), ('qr', 1, 0, 1, 2, 3), ('tanh', 15, 0), ('tanh', 15, 1), ('qh', 13), ('mm2', 0, 0), ('wmul', 15), ('qh', 14), ('mm2', 1, 0), ('qh', 15), ('gain', 0, 0), ('rintA', 2, 2), ('rintA', 2, 3), ('mm2', 0, 1), ('rintV', 2, 0), ('rintV', 2, 1), ('qr', 2, 0, 1, 2, 3), ('gain', 1, 0), ('mm2', 1, 1), ('cast', 0, 0), ('gain', 0, 1), ('rintA', 3, 1), ('rintA', 3, 2), ('rintA', 3, 3), ('mm2', 2, 0), ('rintV', 3, 0), ('qr', 3, 0, 1, 2, 3), ('cast', 1, 0), ('gain', 1, 1), ('mm2', 2, 1), ('cast', 0, 1), ('gain', 2, 0), ('rintA', 4, 0), ('rintA', 4, 1), ('rintA', 4, 2), ('rintA', 4, 3), ('mm2', 3, 0), ('qr', 4, 0, 1, 2, 3), ('cast', 1, 1), ('gain', 2, 1), ('mm2', 3, 1), ('tr', (0, 0), (1, 0)), ('tr', (0, 1), (1, 1)), ('cast', 2, 0), ('gain', 3, 0), ('rintA', 5, 1), ('rintA', 5, 2), ('rintA', 5, 3), ('mm2', 4, 0), ('rintV', 5, 0), ('qr', 5, 0, 1, 2, 3), ('cast', 2, 1), ('gain', 3, 1), ('mm2', 4, 1), ('trcopy', (0, 0), (1, 0)), ('trcopy', (0, 1), (1, 1)), ('cast', 3, 0), ('gain', 4, 0), ('mm2', 5, 0), ('rintV', 6, 0), ('rintV', 6, 1), ('rintV', 6, 2), ('rintV', 6, 3), ('qr', 6, 0, 1, 2, 3), ('cast', 3, 1), ('gain', 4, 1), ('mm2', 5, 1), ('qy', 0, 0), ('qy', 1, 0), ('qy', 0, 1), ('qy', 1, 1), ('tr', (2, 0), (2, 1)), ('tr', (3, 0), (3, 1)), ('cast', 4, 0), ('gain', 5, 0), ('rintA', 7, 1), ('rintA', 7, 2), ('rintA', 7, 3), ('mm2', 6, 0), ('rintV', 7, 0), ('qr', 7, 0, 1, 2, 3), ('cast', 4, 1), ('gain', 5, 1), ('mm2', 6, 1), ('trcopy', (2, 0), (2, 1)), ('trcopy', (3, 0), (3, 1)), ('cast', 5, 0), ('gain', 6, 0), ('mm2', 7, 0), ('cast', 5, 1), ('gain', 6, 1), ('mm2', 7, 1), ('qy', 2, 0), ('qy', 2, 1), ('qy', 3, 0), ('qy', 3, 1), ('tr', (4, 0), (4, 1)), ('tr', (5, 0), (5, 1)), ('cast', 6, 0), ('gain', 7, 0), ('castV', 6, 1), ('gain', 7, 1), ('trcopy', (4, 0), (4, 1)), ('trcopy', (5, 0), (5, 1)), ('tr', (6, 0), (6, 1)), ('castV', 7, 0), ('castV', 7, 1), ('trcopy', (6, 0), (6, 1)), ('qy', 4, 0), ('qy', 4, 1), ('qy', 5, 0), ('qy', 5, 1), ('tr', (7, 0), (7, 1)), ('trcopy', (7, 0), (7, 1)), ('qy', 6, 0), ('qy', 6, 1), ('qy', 7, 0), ('qy', 7, 1)]
+PLAN = [('xperm', 0), ('xsperm', 0), ('mm1', 0, 0), ('tanh', 0, 0), ('xsperm', 1), ('swperm',), ('xperm', 1), ('xperm', 2), ('mm1', 0, 1), ('tanh', 0, 1), ('swturn',), ('wmul', 0, 0, 2), ('mm1', 0, 2), ('tanh', 0, 2), ('mm1', 0, 3), ('tanh', 0, 3), ('wmul', 0, 2, 4), ('qh', 0, 0, 2), ('mm1', 1, 0), ('tanh', 1, 0), ('mm1', 1, 1), ('tanh', 1, 1), ('wmul', 1, 0, 2), ('qh', 0, 2, 4), ('mm1', 1, 2), ('tanh', 1, 2), ('mm1', 1, 3), ('tanh', 1, 3), ('wmul', 1, 2, 4), ('qh', 1, 0, 2), ('mm1', 2, 0), ('tanh', 2, 0), ('mm1', 2, 1), ('tanh', 2, 1), ('qh', 1, 2, 4), ('mm1', 2, 2), ('tanh', 2, 2), ('mm1', 2, 3), ('tanh', 2, 3), ('wmul', 2, 0, 4), ('mm1', 3, 0), ('tanh', 3, 0), ('mm1', 3, 1), ('tanh', 3, 1), ('mm1', 3, 2), ('tanh', 3, 2), ('mm1', 3, 3), ('tanh', 3, 3), ('wmul', 3, 0, 4), ('qh', 2, 0, 4), ('mm1', 4, 0), ('tanh', 4, 0), ('mm1', 4, 1), ('tanh', 4, 1), ('mm1', 4, 2), ('tanh', 4, 2), ('mm1', 4, 3), ('tanh', 4, 3), ('wmul', 4, 0, 4), ('qh', 3, 0, 4), ('mm1', 5, 0), ('tanh', 5, 0), ('mm1', 5, 1), ('tanh', 5, 1), ('mm1', 5, 2), ('tanh', 5, 2), ('mm1', 5, 3), ('tanh', 5, 3), ('wmul', 5, 0, 4), ('qh', 4, 0, 4), ('mm1', 6, 0), ('tanh', 6, 0), ('mm1', 6, 1), ('tanh', 6, 1), ('mm1', 6, 2), ('tanh', 6, 2), ('mm1', 6, 3), ('tanh', 6, 3), ('wmul', 6, 0, 4), ('rintA', 0, 0, 4), ('qh', 5, 0, 4), ('mm1', 7, 0), ('tanh', 7, 0), ('mm1', 7, 1), ('tanh', 7, 1), ('mm1', 7, 2), ('tanh', 7, 2), ('qr', 0), ('rintV', 1, 0, 1), ('mm1', 7, 3), ('tanh', 7, 3), ('wmul', 7, 0, 4), ('rintA', 1, 1, 4), ('qr', 1), ('mm2', 0, 0), ('qh', 6, 0, 4), ('mm2', 1, 0), ('qh', 7, 0, 4), ('rintA', 3, 1, 4), ('mm2', 0, 1), ('rintA', 2, 2, 4), ('rintA', 5, 1, 4), ('rintV', 2, 0, 2), ('rintA', 4, 0, 4), ('mm2', 1, 1), ('qr', 2), ('rintV', 3, 0, 1), ('gain', 0, 0), ('qr', 3), ('mm2', 2, 0), ('gain', 1, 0), ('gain', 0, 1), ('mm2', 3, 0), ('gain', 1, 1), ('cast', 0, 0, 2), ('mm2', 2, 1), ('gain', 2, 0), ('mm2', 3, 1), ('qr', 4), ('rintV', 5, 0, 1), ('gain', 3, 0), ('cast', 1, 0, 2), ('qr', 5), ('mm2', 4, 0), ('rintA', 6, 1, 4), ('tr', 0, 0, 2), ('tr', 1, 0, 2), ('gain', 2, 1), ('mm2', 5, 0), ('gain', 3, 1), ('cast', 2, 0, 2), ('mm2', 4, 1), ('gain', 4, 0), ('rintV', 6, 0, 1), ('mm2', 5, 1), ('trcopy', 0, 0, 2), ('trcopy', 1, 0, 2), ('qr', 6), ('rintV', 7, 0, 4), ('gain', 5, 0), ('cast', 3, 0, 2), ('qr', 7), ('mm2', 6, 0), ('tr', 2, 0, 2), ('tr', 3, 0, 2), ('qy', 0, 0, 2), ('qy', 1, 0, 2), ('gain', 4, 1), ('mm2', 7, 0), ('gain', 5, 1), ('cast', 4, 0, 2), ('mm2', 6, 1), ('gain', 6, 0), ('mm2', 7, 1), ('trcopy', 2, 0, 2), ('trcopy', 3, 0, 2), ('gain', 7, 0), ('cast', 5, 0, 2), ('tr', 4, 0, 2), ('tr', 5, 0, 2), ('qy', 2, 0, 2), ('qy', 3, 0, 2), ('gain', 6, 1), ('castV', 7, 0, 1), ('castD', 7, 1, 2), ('gain', 7, 1), ('cast', 6, 0, 2), ('trcopy', 4, 0, 2), ('trcopy', 5, 0, 2), ('tr', 6, 0, 2), ('trcopy', 6, 0, 2), ('qy', 4, 0, 2), ('qy', 5, 0, 2), ('qy', 6, 0, 2), ('tr', 7, 0, 1), ('trcopy', 7, 0, 1), ('tr', 7, 1, 2), ('trcopy', 7, 1, 2), ('qy', 7, 0, 1), ('qy', 7, 1, 2)]
 
 
 def tile_tanh_cross_moment_planes_h2_kernel(
@@ -34,11 +33,12 @@ def tile_tanh_cross_moment_planes_h2_kernel(
         psum = ctx.enter_context(tc.psum_pool(name="psum", bufs=1))
         ctx.enter_context(tc.manual_schedule())
 
-        x_raw = keep.tile([P, NSG, 2, 512], I32, align_bytes=64)
-        xs_first = keep.tile([P, 2, 128], I32, align_bytes=64)
-        xs_rest = keep.tile([P, 2, 384], I32, align_bytes=64)
-        x_codes = keep.tile([P, NSG, 4, 2, P], I32, align_bytes=64)
-        x_scl = keep.tile([P, NSG, 4, 2, 32], I32, align_bytes=64)
+        x_first = keep.tile([P, 2, 512], I32, align_bytes=64)
+        x_second = keep.tile([P, 2, 512], I32, align_bytes=64)
+        x_rest = keep.tile([P, 2, 1024], I32, align_bytes=64)
+        xs_raw = keep.tile([P, 2, 512], I32, align_bytes=64)
+        x_codes = [keep.tile([P, 2, 4, P * n], I32, name="x_codes%d" % i, align_bytes=64) for i, n in enumerate((1, 1, 2))]
+        x_scl = [keep.tile([P, 2, 4, 32 * n], I32, name="x_scl%d" % i, align_bytes=64) for i, n in enumerate((1, 3))]
         w_codes = keep.tile([P, 2, 512], I32, align_bytes=64)
         w_scl = keep.tile([P, 2, 256], I32, align_bytes=64)
         r_raw = keep.tile([P, NSG, 4, F], BF16, align_bytes=64)
@@ -52,7 +52,7 @@ def tile_tanh_cross_moment_planes_h2_kernel(
         h_scl = keep.tile([P, NSG, C], U8, align_bytes=64)
         r_codes = keep.tile([P, NFT, NSG, P], I32, align_bytes=64)
         r_scl = keep.tile([P, NFT, NSG, P], U8, align_bytes=64)
-        y_codes = keep.tile([P, 2, F], I32, align_bytes=64)
+        y_codes = keep.tile([P, 4, 2, 2 * P], I32, align_bytes=64)
         y_scl = keep.tile([P, 2, F], U8, align_bytes=64)
 
         xw = x_words.rearrange("g p n t -> p g (n t)").bitcast(I32)
@@ -62,25 +62,21 @@ def tile_tanh_cross_moment_planes_h2_kernel(
         o1 = out_1.rearrange("g p m t -> p g (m t)").bitcast(I32)
         o2 = out_2.rearrange("g q n -> q g n").bitcast(I32)
 
-        nc.vector.memset(xs_first[:], 0)
+        for q in range(4):
+            nc.sync.dma_start(out=xs_raw[32 * q : 32 * q + 4], in_=xs[4 * q : 4 * q + 4])
+        nc.scalar.dma_start(out=x_first[:], in_=xw[:, :, 0:512])
+        nc.scalar.dma_start(out=w_codes[:], in_=ww)
         nc.vector.memset(w_scl[:], 0)
         nc.vector.memset(warm[:], 0.0)
-        nc.vector.memset(xs_rest[:], 0)
+        nc.vector.memset(x_scl[0][:], 0)
+        nc.vector.memset(x_scl[1][:], 0)
         nc.vector.memset(sw_rows[:], 0.0)
-        nc.sync.dma_start(out=x_raw[:, 0], in_=xw[:, :, 0:512])
-        nc.scalar.dma_start(out=w_codes[:], in_=ww)
         for q in range(4):
-            nc.sync.dma_start(out=xs_first[32 * q : 32 * q + 4], in_=xs[4 * q : 4 * q + 4, :, 0:128])
-        for q in range(4):
-            eng = nc.scalar if q < 2 else nc.sync
-            eng.dma_start(out=w_scl[32 * q : 32 * q + 4], in_=ws[4 * q : 4 * q + 4])
+            nc.sync.dma_start(out=w_scl[32 * q : 32 * q + 4], in_=ws[4 * q : 4 * q + 4])
         nc.scalar.activation(out=warm[:, 4:8], in_=warm[:, 0:4], func=ACT.Tanh)
         nc.sync.dma_start(out=sw_raw[:], in_=sample_weight.rearrange("(s n) -> s n", s=NSG))
-        nc.sync.dma_start(out=x_raw[:, 1], in_=xw[:, :, 512:1024])
-        for q in range(4):
-            nc.sync.dma_start(out=xs_rest[32 * q : 32 * q + 4], in_=xs[4 * q : 4 * q + 4, :, 128:512])
-        for sg in range(2, NSG):
-            nc.sync.dma_start(out=x_raw[:, sg], in_=xw[:, :, 512 * sg : 512 * (sg + 1)])
+        nc.sync.dma_start(out=x_second[:], in_=xw[:, :, 512:1024])
+        nc.sync.dma_start(out=x_rest[:], in_=xw[:, :, 1024:S])
         for sg in range(NSG):
             rows = x_rows[512 * sg : 512 * (sg + 1), :].rearrange("(j t r) f -> r j t f", t=4, r=4)
             for r in range(4):
@@ -88,20 +84,23 @@ def tile_tanh_cross_moment_planes_h2_kernel(
         nc.sync.dma_start(out=gain_all[:], in_=gain.partition_broadcast(P))
         make_identity(nc, ident[:])
 
-        z_bank, t_tile, h_tile, r_tile, acc_bank, y_tile, yb_tile, tr_bank, yw_of = {}, {}, {}, {}, {}, {}, {}, {}, {}
+        z_bank, t_tile, h_tile, r_tile, acc_bank, y_tile, yb_tile, tr_bank, yw_tile = {}, {}, {}, {}, {}, {}, {}, {}, {}
         count = {"z": 0, "acc": 0, "tr": 0}
 
-        def xperm(sg):
+        def xperm(part):
+            src = (x_first, x_second, x_rest)[part]
             nc.vector.tensor_copy(
-                out=x_codes[:, sg].rearrange("p t g (j r) -> p t (g j) r", r=4),
-                in_=x_raw[:, sg].rearrange("p g (j t r) -> p t (g j) r", t=4, r=4),
+                out=x_codes[part][:].rearrange("p g t (j r) -> p g t j r", r=4),
+                in_=src[:].rearrange("p g (j t r) -> p g t j r", t=4, r=4),
             )
 
-        def xsperm(sg):
-            nc.vector.tensor_copy(
-                out=x_scl[:, sg],
-                in_=(xs_first[:] if sg == 0 else xs_rest[:, :, 128 * (sg - 1) : 128 * sg]).rearrange("p g (j t) -> p t g j", t=4),
-            )
+        def xsperm(part):
+            lo, hi = ((0, 128), (128, 512))[part]
+            for q in range(4):
+                rows = slice(32 * q, 32 * q + 4)
+                nc.vector.tensor_copy(
+                    out=x_scl[part][rows], in_=xs_raw[rows, :, lo:hi].rearrange("p g (j t) -> p g t j", t=4)
+                )
 
         def swperm():
             nc.vector.tensor_copy(
@@ -115,59 +114,61 @@ def tile_tanh_cross_moment_planes_h2_kernel(
                 nc.tensor.transpose(bank[:, t, :], sw_rows[:, t, :], ident[:])
             nc.scalar.copy(out=sw[:], in_=bank[:, :, 0:NSG].rearrange("p t s -> p s t"))
 
-        def mm1(k, h):
-            sg, c0 = (k // 2) % 4, 512 * (k // 8) + 256 * (k % 2) + 128 * h
-            bank = psum.tile([P, 4, P], F32, name="bank%d" % (count["z"] % 3))
+        def mm1(grp, b):
+            sg, c0 = grp % 4, 512 * (grp // 4) + P * b
+            bank = psum.tile([P, 4, P], F32, name="bank%d" % (count["z"] % 5))
             count["z"] += 1
-            z_bank[k, h] = bank
+            z_bank[grp, b] = bank
+            codes, c_at = x_codes[min(sg, 2)], max(sg - 2, 0)
+            scl, s_at = x_scl[min(sg, 1)], max(sg - 1, 0)
             for t in range(4):
                 for g in range(2):
                     nc.tensor.matmul_mx(
                         out=bank[:, t, :],
-                        lhsT=x_codes[:, sg, t, g, :].bitcast(FP8X4),
-                        lhsT_scale=x_scl[:, sg, t, g, :].bitcast(U8),
+                        lhsT=codes[:, g, t, P * c_at : P * (c_at + 1)].bitcast(FP8X4),
+                        lhsT_scale=scl[:, g, t, 32 * s_at : 32 * (s_at + 1)].bitcast(U8),
                         rhs=w_codes[:, g, c0 // 2 : c0 // 2 + 64].bitcast(U8).bitcast(FP4X4),
                         rhs_scale=w_scl[:, g, c0 // 4 : c0 // 4 + 32].bitcast(U8),
                         start=(g == 0),
                         stop=(g == 1),
                     )
 
-        def tanh(k, h):
-            if h == 0:
-                t_tile[k] = work.tile([P, 256, 4], F32, name="tanh_z", bufs=5, align_bytes=64)
+        def tanh(grp, b):
+            if b == 0:
+                t_tile[grp] = work.tile([P, 512, 4], F32, name="tanh_z", align_bytes=64)
             nc.scalar.activation(
-                out=t_tile[k][:, 128 * h : 128 * (h + 1), :],
-                in_=z_bank[k, h][:].rearrange("p t n -> p n t"),
+                out=t_tile[grp][:, P * b : P * (b + 1), :],
+                in_=z_bank[grp, b][:].rearrange("p t n -> p n t"),
                 func=ACT.Tanh,
             )
 
-        def wmul(k):
-            sg = (k // 2) % 4
-            h_tile[k] = work.tile([P, 256, 4], BF16, name="h_bf", align_bytes=64)
+        def wmul(grp, b0, b1):
+            if b0 == 0:
+                h_tile[grp] = work.tile([P, 512, 4], BF16, name="h_bf", align_bytes=64)
             nc.vector.tensor_tensor(
-                out=h_tile[k][:],
-                in0=t_tile[k][:],
-                in1=sw[:, sg, :].unsqueeze(1).to_broadcast([P, 256, 4]),
+                out=h_tile[grp][:, P * b0 : P * b1, :],
+                in0=t_tile[grp][:, P * b0 : P * b1, :],
+                in1=sw[:, grp % 4, :].unsqueeze(1).to_broadcast([P, P * (b1 - b0), 4]),
                 op=ALU.mult,
             )
 
-        def qh(k):
-            sg, c0 = (k // 2) % 4, 512 * (k // 8) + 256 * (k % 2)
+        def qh(grp, b0, b1):
+            cols = slice(512 * (grp // 4) + P * b0, 512 * (grp // 4) + P * b1)
             nc.vector.quantize_mx(
-                out=h_codes[:, sg, c0 : c0 + 256].bitcast(FP8X4),
-                scales=h_scl[:, sg, c0 : c0 + 256],
-                in_=h_tile[k][:].rearrange("p n t -> p (n t)"),
+                out=h_codes[:, grp % 4, cols].bitcast(FP8X4),
+                scales=h_scl[:, grp % 4, cols],
+                in_=h_tile[grp][:, P * b0 : P * b1, :].rearrange("p n t -> p (n t)"),
             )
 
-        def rint(ft, sg, copy):
+        def rint(ft, s0, s1, copy):
             if ft not in r_tile:
                 r_tile[ft] = work.tile([P, NSG, P, 4], BF16, name="r_bf", align_bytes=64, bufs=RB)
             copy(
-                out=r_tile[ft][:, sg].rearrange("p (c i) t -> p c t i", i=4),
-                in_=r_raw[:, sg, :, P * ft : P * (ft + 1)].rearrange("p t (c i) -> p c t i", i=4),
+                out=r_tile[ft][:, s0:s1].rearrange("p s (c i) t -> p s c t i", i=4),
+                in_=r_raw[:, s0:s1, :, P * ft : P * (ft + 1)].rearrange("p s t (c i) -> p s c t i", i=4),
             )
 
-        def qr(ft, *unused):
+        def qr(ft):
             nc.vector.quantize_mx(
                 out=r_codes[:, ft].rearrange("p s f -> p (s f)").bitcast(FP8X4),
                 scales=r_scl[:, ft].rearrange("p s f -> p (s f)"),
@@ -175,7 +176,7 @@ def tile_tanh_cross_moment_planes_h2_kernel(
             )
 
         def mm2(ft, ch):
-            bank = psum.tile([P, 512], F32, name="bank%d" % (3 + count["acc"] % AB))
+            bank = psum.tile([P, 512], F32, name="bank%d" % (3 + (count["acc"] + 2) % 5))
             count["acc"] += 1
             acc_bank[ft, ch] = bank
             for sg in range(NSG):
@@ -190,61 +191,82 @@ def tile_tanh_cross_moment_planes_h2_kernel(
                 )
 
         def scale_out(ft, ch):
-            y = work.tile([P, 512], F32, name="y", bufs=6, align_bytes=64)
-            y_tile[ft, ch] = y
+            j, i = 2 * (ft // 2) + ch, ft % 2
+            if i == 0:
+                y_tile[j] = work.tile([P, 2, 512], F32, name="y", bufs=4, align_bytes=64)
+            cols = slice(512 * ch, 512 * (ch + 1))
             nc.vector.scalar_tensor_tensor(
-                out=y[:],
-                in0=acc_bank[ft, ch][:],
-                scalar=1.0 / S,
-                in1=gain_all[:, 512 * ch : 512 * (ch + 1)],
-                op0=ALU.mult,
-                op1=ALU.mult,
+                out=y_tile[j][:, i, :], in0=acc_bank[ft, ch][:], scalar=1.0 / S, in1=gain_all[:, cols],
+                op0=ALU.mult, op1=ALU.mult,
             )
-            nc.sync.dma_start(out=out_0[P * ft : P * (ft + 1), 512 * ch : 512 * (ch + 1)], in_=y[:])
+            if j == 7:
+                nc.sync.dma_start(out=out_0[P * ft : P * (ft + 1), cols], in_=y_tile[j][:, i, :])
+            elif i == 1:
+                nc.sync.dma_start(
+                    out=out_0[P * (ft - 1) : P * (ft + 1), cols].rearrange("(i p) c -> p i c", i=2), in_=y_tile[j][:]
+                )
 
-        def cast(ft, ch, copy):
-            yb = work.tile([P, 2, P, 2], BF16, name="y_bf", bufs=6, align_bytes=64)
-            yb_tile[ft, ch] = yb
-            copy(out=yb[:], in_=y_tile[ft, ch][:].rearrange("p (q u e) -> p u q e", u=2, e=2))
+        def yb_of(j):
+            if j not in yb_tile:
+                yb_tile[j] = work.tile([P, 2, 2, P, 2], BF16, name="y_bf", bufs=4, align_bytes=64)
+            return yb_tile[j]
 
-        def tr(*units):
+        def cast(j, i0, i1, copy):
+            copy(out=yb_of(j)[:, i0:i1], in_=y_tile[j][:, i0:i1].rearrange("p i (q u e) -> p i u q e", u=2, e=2))
+
+        def cast_direct(j, i0, i1):
+            ft, ch = 2 * (j // 2) + i0, j % 2
+            acc = acc_bank[ft, ch][:].rearrange("p (q u e) -> p u q e", u=2, e=2)
+            gv = gain_all[:, 512 * ch : 512 * (ch + 1)].rearrange("p (q u e) -> p u q e", u=2, e=2)
+            for u in range(2):
+                nc.vector.scalar_tensor_tensor(
+                    out=yb_of(j)[:, i0, u], in0=acc[:, u], scalar=1.0 / S, in1=gv[:, u], op0=ALU.mult, op1=ALU.mult
+                )
+
+        def tr(j, i0, i1):
             bank = psum.tile([P, 2, 2, P], F32, name="bank%d" % (count["tr"] % 3))
             count["tr"] += 1
-            tr_bank[units] = bank
-            for i, unit in enumerate(units):
-                words = yb_tile[unit][:].rearrange("p u q e -> p u (q e)").bitcast(F32)
+            tr_bank[j, i0] = bank
+            words = yb_tile[j][:].rearrange("p i u q e -> p i u (q e)").bitcast(F32)
+            for i in range(i0, i1):
                 for u in range(2):
-                    nc.tensor.transpose(bank[:, i, u, :], words[:, u, :], ident[:])
+                    nc.tensor.transpose(bank[:, i, u, :], words[:, i, u, :], ident[:])
 
-        def trcopy(*units):
-            n = len(units)
+        def trcopy(j, i0, i1, copy):
             yw = work.tile([P, 2, P, 2], F32, name="y_words", bufs=4, align_bytes=64)
-            nc.scalar.copy(out=yw[:, :n], in_=tr_bank[units][:, :n].rearrange("p i u f -> p i f u"))
-            for i, unit in enumerate(units):
-                yw_of[unit] = yw[:, i].rearrange("p f u -> p (f u)").bitcast(BF16)
+            yw_tile[j, i0] = yw
+            copy(out=yw[:, i0:i1], in_=tr_bank[j, i0][:, i0:i1].rearrange("p i u f -> p i f u"))
 
-        done_y = set()
-
-        def qy(ft, ch):
+        def qy(j, i0, i1):
+            f0, ch = 2 * P * (j // 2), j % 2
+            cols = slice(f0 + P * i0, f0 + P * i1)
             nc.vector.quantize_mx(
-                out=y_codes[:, ch, P * ft : P * (ft + 1)].bitcast(FP8X4),
-                scales=y_scl[:, ch, P * ft : P * (ft + 1)],
-                in_=yw_of[ft, ch],
+                out=y_codes[:, j // 2, ch, P * i0 : P * i1].bitcast(FP8X4),
+                scales=y_scl[:, ch, cols],
+                in_=yw_tile[j, i0][:, i0:i1].rearrange("p i f u -> p (i f u)").bitcast(BF16),
             )
-            done_y.add((ft, ch))
-            for lo, hi in WSTORE:
-                if lo <= ft < hi and all((f, c) in done_y for f in range(lo, hi) for c in range(2)):
-                    nc.sync.dma_start(out=o1[:, :, P * lo : P * hi], in_=y_codes[:, :, P * lo : P * hi])
-            if len(done_y) == 2 * NFT:
+            pair = slice(f0, f0 + 2 * P)
+            if j >= 6 and i1 == 2:
+                nc.sync.dma_start(out=o1[:, ch, pair], in_=y_codes[:, j // 2, ch])
+            elif j < 6 and ch == 1:
+                nc.sync.dma_start(out=o1[:, :, pair], in_=y_codes[:, j // 2])
+            if j == 7 and i1 == 2:
                 for q in range(4):
                     eng = nc.sync if q % 2 == 0 else nc.scalar
                     eng.dma_start(out=o2[4 * q : 4 * q + 4], in_=y_scl[32 * q : 32 * q + 4].bitcast(I32))
 
         steps = {
-            "swperm": swperm, "swturn": swturn, "xperm": xperm, "xsperm": xsperm, "mm1": mm1, "tanh": tanh, "wmul": wmul, "qh": qh,
-            "rintA": lambda ft, sg: rint(ft, sg, nc.scalar.copy),
-            "rintV": lambda ft, sg: rint(ft, sg, nc.vector.tensor_copy),
-            "qr": qr, "mm2": mm2, "gain": scale_out, "cast": lambda ft, ch: cast(ft, ch, nc.scalar.copy), "castV": lambda ft, ch: cast(ft, ch, nc.vector.tensor_copy), "tr": tr, "trcopy": trcopy, "qy": qy,
+            "swperm": swperm, "swturn": swturn, "xperm": xperm, "xsperm": xsperm, "mm1": mm1, "tanh": tanh,
+            "wmul": wmul, "qh": qh,
+            "rintA": lambda *a: rint(*a, nc.scalar.copy),
+            "rintV": lambda *a: rint(*a, nc.vector.tensor_copy),
+            "qr": qr, "mm2": mm2, "gain": scale_out,
+            "cast": lambda *a: cast(*a, nc.scalar.copy),
+            "castV": lambda *a: cast(*a, nc.vector.tensor_copy),
+            "castD": cast_direct, "tr": tr,
+            "trcopy": lambda *a: trcopy(*a, nc.scalar.copy),
+            "trcopyV": lambda *a: trcopy(*a, nc.vector.tensor_copy),
+            "qy": qy,
         }
         for step in PLAN:
             steps[step[0]](*step[1:])

@@ -16,11 +16,20 @@ ACT = mybir.ActivationFunctionType
 ALU = mybir.AluOpType
 
 P = 128
-NSG = 4
-NFT = 8
-RB = 8
+SLOTS = 4
+K_PASS = P * SLOTS
+GROUPS = S // K_PASS
+F_TILES = F // P
+ALIGN = 64
 
-PLAN = [('xperm', 0), ('xsperm', 0), ('mm1', 0, 0), ('tanh', 0, 0), ('xsperm', 1), ('swperm',), ('xperm', 1), ('xperm', 2), ('mm1', 0, 1), ('tanh', 0, 1), ('swturn',), ('wmul', 0, 0, 2), ('mm1', 0, 2), ('tanh', 0, 2), ('mm1', 0, 3), ('tanh', 0, 3), ('wmul', 0, 2, 4), ('qh', 0, 0, 2), ('mm1', 1, 0), ('tanh', 1, 0), ('mm1', 1, 1), ('tanh', 1, 1), ('wmul', 1, 0, 2), ('qh', 0, 2, 4), ('mm1', 1, 2), ('tanh', 1, 2), ('mm1', 1, 3), ('tanh', 1, 3), ('wmul', 1, 2, 4), ('qh', 1, 0, 2), ('mm1', 2, 0), ('tanh', 2, 0), ('mm1', 2, 1), ('tanh', 2, 1), ('qh', 1, 2, 4), ('mm1', 2, 2), ('tanh', 2, 2), ('mm1', 2, 3), ('tanh', 2, 3), ('wmul', 2, 0, 4), ('mm1', 3, 0), ('tanh', 3, 0), ('mm1', 3, 1), ('tanh', 3, 1), ('mm1', 3, 2), ('tanh', 3, 2), ('mm1', 3, 3), ('tanh', 3, 3), ('wmul', 3, 0, 4), ('qh', 2, 0, 4), ('mm1', 4, 0), ('tanh', 4, 0), ('mm1', 4, 1), ('tanh', 4, 1), ('mm1', 4, 2), ('tanh', 4, 2), ('mm1', 4, 3), ('tanh', 4, 3), ('wmul', 4, 0, 4), ('qh', 3, 0, 4), ('mm1', 5, 0), ('tanh', 5, 0), ('mm1', 5, 1), ('tanh', 5, 1), ('mm1', 5, 2), ('tanh', 5, 2), ('mm1', 5, 3), ('tanh', 5, 3), ('wmul', 5, 0, 4), ('qh', 4, 0, 4), ('mm1', 6, 0), ('tanh', 6, 0), ('mm1', 6, 1), ('tanh', 6, 1), ('mm1', 6, 2), ('tanh', 6, 2), ('mm1', 6, 3), ('tanh', 6, 3), ('wmul', 6, 0, 4), ('rintA', 0, 0, 4), ('qh', 5, 0, 4), ('mm1', 7, 0), ('tanh', 7, 0), ('mm1', 7, 1), ('tanh', 7, 1), ('mm1', 7, 2), ('tanh', 7, 2), ('qr', 0), ('rintV', 1, 0, 1), ('mm1', 7, 3), ('tanh', 7, 3), ('wmul', 7, 0, 4), ('rintA', 1, 1, 4), ('qr', 1), ('mm2', 0, 0), ('qh', 6, 0, 4), ('mm2', 1, 0), ('qh', 7, 0, 4), ('rintA', 3, 1, 4), ('mm2', 0, 1), ('rintA', 2, 2, 4), ('rintA', 5, 1, 4), ('rintV', 2, 0, 2), ('rintA', 4, 0, 4), ('mm2', 1, 1), ('qr', 2), ('rintV', 3, 0, 1), ('gain', 0, 0), ('qr', 3), ('mm2', 2, 0), ('gain', 1, 0), ('gain', 0, 1), ('mm2', 3, 0), ('gain', 1, 1), ('cast', 0, 0, 2), ('mm2', 2, 1), ('gain', 2, 0), ('mm2', 3, 1), ('qr', 4), ('rintV', 5, 0, 1), ('gain', 3, 0), ('cast', 1, 0, 2), ('qr', 5), ('mm2', 4, 0), ('rintA', 6, 1, 4), ('tr', 0, 0, 2), ('tr', 1, 0, 2), ('gain', 2, 1), ('mm2', 5, 0), ('gain', 3, 1), ('cast', 2, 0, 2), ('mm2', 4, 1), ('gain', 4, 0), ('rintV', 6, 0, 1), ('mm2', 5, 1), ('trcopy', 0, 0, 2), ('trcopy', 1, 0, 2), ('qr', 6), ('rintV', 7, 0, 4), ('gain', 5, 0), ('cast', 3, 0, 2), ('qr', 7), ('mm2', 6, 0), ('tr', 2, 0, 2), ('tr', 3, 0, 2), ('qy', 0, 0, 2), ('qy', 1, 0, 2), ('gain', 4, 1), ('mm2', 7, 0), ('gain', 5, 1), ('cast', 4, 0, 2), ('mm2', 6, 1), ('gain', 6, 0), ('mm2', 7, 1), ('trcopy', 2, 0, 2), ('trcopy', 3, 0, 2), ('gain', 7, 0), ('cast', 5, 0, 2), ('tr', 4, 0, 2), ('tr', 5, 0, 2), ('qy', 2, 0, 2), ('qy', 3, 0, 2), ('gain', 6, 1), ('castV', 7, 0, 1), ('castD', 7, 1, 2), ('gain', 7, 1), ('cast', 6, 0, 2), ('trcopy', 4, 0, 2), ('trcopy', 5, 0, 2), ('tr', 6, 0, 2), ('trcopy', 6, 0, 2), ('qy', 4, 0, 2), ('qy', 5, 0, 2), ('qy', 6, 0, 2), ('tr', 7, 0, 1), ('trcopy', 7, 0, 1), ('tr', 7, 1, 2), ('trcopy', 7, 1, 2), ('qy', 7, 0, 1), ('qy', 7, 1, 2)]
+Z_BANKS = 4
+WEIGHT_BANK = 7
+Y_BANKS = [4, 5, 6, 0, 1, 2, 3, 7, 4, 5, 6, 3, 7, 4, 5, 6]
+TURN_BANKS = 3
+
+GPSIMD_HALVES = {2: (0, 0), 3: (1, 0), 4: (0, 2), 5: (1, 2), 6: (3, 0), 7: (4, 0)}
+SCALAR_HALVES = {4: (2, 0), 5: (2, 2), 6: (3, 2)}
+SCALAR_HALVES_QUANTISED = {5: (2, 0, 4), 6: (3, 2, 4)}
 
 
 def tile_tanh_cross_moment_planes_h2_kernel(
@@ -33,240 +42,329 @@ def tile_tanh_cross_moment_planes_h2_kernel(
         psum = ctx.enter_context(tc.psum_pool(name="psum", bufs=1))
         ctx.enter_context(tc.manual_schedule())
 
-        x_first = keep.tile([P, 2, 512], I32, align_bytes=64)
-        x_second = keep.tile([P, 2, 512], I32, align_bytes=64)
-        x_rest = keep.tile([P, 2, 1024], I32, align_bytes=64)
-        xs_raw = keep.tile([P, 2, 512], I32, align_bytes=64)
-        x_codes = [keep.tile([P, 2, 4, P * n], I32, name="x_codes%d" % i, align_bytes=64) for i, n in enumerate((1, 1, 2))]
-        x_scl = [keep.tile([P, 2, 4, 32 * n], I32, name="x_scl%d" % i, align_bytes=64) for i, n in enumerate((1, 3))]
-        w_codes = keep.tile([P, 2, 512], I32, align_bytes=64)
-        w_scl = keep.tile([P, 2, 256], I32, align_bytes=64)
-        r_raw = keep.tile([P, NSG, 4, F], BF16, align_bytes=64)
-        sw_raw = keep.tile([NSG, 512], BF16, align_bytes=64)
-        sw_rows = keep.tile([P, 4, P], F32, align_bytes=64)
-        sw = keep.tile([P, NSG, 4], F32, align_bytes=64)
-        gain_all = keep.tile([P, C], BF16, align_bytes=64)
-        ident = keep.tile([P, P], F32, align_bytes=64)
-        warm = keep.tile([P, 8], F32, align_bytes=64)
-        h_codes = keep.tile([P, NSG, C], I32, align_bytes=64)
-        h_scl = keep.tile([P, NSG, C], U8, align_bytes=64)
-        r_codes = keep.tile([P, NFT, NSG, P], I32, align_bytes=64)
-        r_scl = keep.tile([P, NFT, NSG, P], U8, align_bytes=64)
-        y_codes = keep.tile([P, 4, 2, 2 * P], I32, align_bytes=64)
-        y_scl = keep.tile([P, 2, F], U8, align_bytes=64)
+        x_parts, scale_parts = (1, 1, 2), (1, 3)
+        x_raw = [keep.tile([P, 2, K_PASS * n], I32, name="x_raw%d" % i, align_bytes=ALIGN) for i, n in enumerate(x_parts)]
+        x_codes = [keep.tile([P, 2, SLOTS, P * n], I32, name="x_codes%d" % i, align_bytes=ALIGN) for i, n in enumerate(x_parts)]
+        x_scales_raw = keep.tile([P, 2, S // 4], I32, align_bytes=ALIGN)
+        x_planes = [keep.tile([P, 2, SLOTS, P // 4 * n], I32, name="x_plane%d" % i, align_bytes=ALIGN) for i, n in enumerate(scale_parts)]
+        w_codes = keep.tile([P, 2, C // 2], I32, align_bytes=ALIGN)
+        w_plane = keep.tile([P, 2, C // 4], I32, align_bytes=ALIGN)
+        r_raw = keep.tile([P, GROUPS, SLOTS, F], BF16, align_bytes=ALIGN)
+        weight_raw = keep.tile([GROUPS, K_PASS], BF16, align_bytes=ALIGN)
+        weight_rows = keep.tile([P, SLOTS, P], F32, align_bytes=ALIGN)
+        zero = keep.tile([P, 1], F32, align_bytes=ALIGN)
+        gain_rows = keep.tile([P, C], BF16, align_bytes=ALIGN)
+        identity = keep.tile([P, P], F32, align_bytes=ALIGN)
+        h_codes = keep.tile([P, GROUPS, C], I32, align_bytes=ALIGN)
+        h_plane = keep.tile([P, GROUPS, C], U8, align_bytes=ALIGN)
+        r_codes = keep.tile([P, F_TILES, GROUPS, P], I32, align_bytes=ALIGN)
+        r_plane = keep.tile([P, F_TILES, GROUPS, P], U8, align_bytes=ALIGN)
+        y_codes = keep.tile([P, F_TILES // 2, 2, 2 * P], I32, align_bytes=ALIGN)
+        y_plane = keep.tile([P, 2, F], U8, align_bytes=ALIGN)
 
-        xw = x_words.rearrange("g p n t -> p g (n t)").bitcast(I32)
-        ww = w_words.rearrange("g p b -> p g b").bitcast(I32)
-        xs = x_scales.rearrange("g q n -> q g n").bitcast(I32)
-        ws = w_scales.rearrange("g q n -> q g n").bitcast(I32)
-        o1 = out_1.rearrange("g p m t -> p g (m t)").bitcast(I32)
-        o2 = out_2.rearrange("g q n -> q g n").bitcast(I32)
+        x_words_i = x_words.rearrange("g p n t -> p g (n t)").bitcast(I32)
+        w_words_i = w_words.rearrange("g p b -> p g b").bitcast(I32)
+        x_scales_i = x_scales.rearrange("g q n -> q g n").bitcast(I32)
+        w_scales_i = w_scales.rearrange("g q n -> q g n").bitcast(I32)
+        out_words_i = out_1.rearrange("g p m t -> p g (m t)").bitcast(I32)
+        out_scales_i = out_2.rearrange("g q n -> q g n").bitcast(I32)
+        quadrants = [(slice(32 * q, 32 * q + 4), slice(4 * q, 4 * q + 4)) for q in range(4)]
 
-        for q in range(4):
-            nc.sync.dma_start(out=xs_raw[32 * q : 32 * q + 4], in_=xs[4 * q : 4 * q + 4])
-        nc.scalar.dma_start(out=x_first[:], in_=xw[:, :, 0:512])
-        nc.scalar.dma_start(out=w_codes[:], in_=ww)
-        nc.vector.memset(w_scl[:], 0)
-        nc.vector.memset(warm[:], 0.0)
-        nc.vector.memset(x_scl[0][:], 0)
-        nc.vector.memset(x_scl[1][:], 0)
-        nc.vector.memset(sw_rows[:], 0.0)
-        for q in range(4):
-            nc.sync.dma_start(out=w_scl[32 * q : 32 * q + 4], in_=ws[4 * q : 4 * q + 4])
-        nc.scalar.activation(out=warm[:, 4:8], in_=warm[:, 0:4], func=ACT.Tanh)
-        nc.sync.dma_start(out=sw_raw[:], in_=sample_weight.rearrange("(s n) -> s n", s=NSG))
-        nc.sync.dma_start(out=x_second[:], in_=xw[:, :, 512:1024])
-        nc.sync.dma_start(out=x_rest[:], in_=xw[:, :, 1024:S])
-        for sg in range(NSG):
-            rows = x_rows[512 * sg : 512 * (sg + 1), :].rearrange("(j t r) f -> r j t f", t=4, r=4)
+        for live, rows in quadrants:
+            nc.sync.dma_start(out=x_scales_raw[live], in_=x_scales_i[rows])
+        nc.scalar.dma_start(out=x_raw[0][:], in_=x_words_i[:, :, 0:K_PASS])
+        nc.scalar.dma_start(out=w_codes[:], in_=w_words_i)
+        nc.vector.memset(w_plane[:], 0)
+        nc.vector.memset(zero[:], 0.0)
+        for plane in x_planes:
+            nc.vector.memset(plane[:], 0)
+        for live, rows in quadrants:
+            nc.sync.dma_start(out=w_plane[live], in_=w_scales_i[rows])
+        nc.scalar.activation(
+            out=weight_rows[:].rearrange("p t m -> p (t m)"), in_=zero[:].to_broadcast([P, SLOTS * P]), func=ACT.Tanh
+        )
+        nc.sync.dma_start(out=weight_raw[:], in_=sample_weight.rearrange("(s n) -> s n", s=GROUPS))
+        nc.sync.dma_start(out=x_raw[1][:], in_=x_words_i[:, :, K_PASS : 2 * K_PASS])
+        nc.sync.dma_start(out=x_raw[2][:], in_=x_words_i[:, :, 2 * K_PASS : S])
+        for group in range(GROUPS):
+            rows = x_rows[K_PASS * group : K_PASS * (group + 1), :].rearrange("(j t r) f -> r j t f", t=SLOTS, r=4)
             for r in range(4):
-                nc.sync.dma_start(out=r_raw[r:P:4, sg], in_=rows[r])
-        nc.sync.dma_start(out=gain_all[:], in_=gain.partition_broadcast(P))
-        make_identity(nc, ident[:])
+                nc.sync.dma_start(out=r_raw[r:P:4, group], in_=rows[r])
+        nc.sync.dma_start(out=gain_rows[:], in_=gain.partition_broadcast(P))
+        make_identity(nc, identity[:])
 
-        z_bank, t_tile, h_tile, r_tile, acc_bank, y_tile, yb_tile, tr_bank, yw_tile = {}, {}, {}, {}, {}, {}, {}, {}, {}
-        count = {"z": 0, "acc": 0, "tr": 0}
+        tanh_tiles, h_tiles, r_tiles, r_halves = {}, {}, {}, {}
+        y_banks, y_tiles, y_bf_tiles, turned, y_word_tiles = {}, {}, {}, {}, {}
 
-        def xperm(part):
-            src = (x_first, x_second, x_rest)[part]
+        def bank_tile(shape, bank):
+            return psum.tile(shape, F32, name="bank%d" % bank)
+
+        def gpsimd_copy(out, in_):
+            nc.gpsimd.tensor_scalar(out=out, in0=in_, scalar1=1.0, scalar2=0.0, op0=ALU.mult, op1=ALU.add)
+
+        def reorder_x(part):
             nc.vector.tensor_copy(
                 out=x_codes[part][:].rearrange("p g t (j r) -> p g t j r", r=4),
-                in_=src[:].rearrange("p g (j t r) -> p g t j r", t=4, r=4),
+                in_=x_raw[part][:].rearrange("p g (j t r) -> p g t j r", t=SLOTS, r=4),
             )
 
-        def xsperm(part):
-            lo, hi = ((0, 128), (128, 512))[part]
-            for q in range(4):
-                rows = slice(32 * q, 32 * q + 4)
+        def reorder_x_scales(part):
+            lo = P * sum(scale_parts[:part])
+            for live, rows in quadrants:
                 nc.vector.tensor_copy(
-                    out=x_scl[part][rows], in_=xs_raw[rows, :, lo:hi].rearrange("p g (j t) -> p g t j", t=4)
+                    out=x_planes[part][live],
+                    in_=x_scales_raw[live, :, lo : lo + P * scale_parts[part]].rearrange("p g (j t) -> p g t j", t=SLOTS),
                 )
 
-        def swperm():
+        def reorder_weights():
             nc.vector.tensor_copy(
-                out=sw_rows[0:NSG].rearrange("s t (j r) -> s t j r", r=4),
-                in_=sw_raw[:].rearrange("s (j t r) -> s t j r", t=4, r=4),
+                out=weight_rows[0:GROUPS].rearrange("s t (j r) -> s t j r", r=4),
+                in_=weight_raw[:].rearrange("s (j t r) -> s t j r", t=SLOTS, r=4),
             )
 
-        def swturn():
-            bank = psum.tile([P, 4, P], F32, name="bank7")
-            for t in range(4):
-                nc.tensor.transpose(bank[:, t, :], sw_rows[:, t, :], ident[:])
-            nc.scalar.copy(out=sw[:], in_=bank[:, :, 0:NSG].rearrange("p t s -> p s t"))
+        def turn_weights():
+            bank = bank_tile([P, SLOTS, P], WEIGHT_BANK)
+            for t in range(SLOTS):
+                nc.tensor.transpose(bank[:, t, :], weight_rows[:, t, :], identity[:])
+            return bank
 
-        def mm1(grp, b):
-            sg, c0 = grp % 4, 512 * (grp // 4) + P * b
-            bank = psum.tile([P, 4, P], F32, name="bank%d" % (count["z"] % 5))
-            count["z"] += 1
-            z_bank[grp, b] = bank
-            codes, c_at = x_codes[min(sg, 2)], max(sg - 2, 0)
-            scl, s_at = x_scl[min(sg, 1)], max(sg - 1, 0)
-            for t in range(4):
+        def tanh_quarter(block, b):
+            group, c0 = block % GROUPS, K_PASS * (block // GROUPS) + P * b
+            codes, codes_at = x_codes[min(group, 2)], P * max(group - 2, 0)
+            plane, plane_at = x_planes[min(group, 1)], P // 4 * max(group - 1, 0)
+            bank = bank_tile([P, SLOTS, P], (4 * block + b) % Z_BANKS)
+            for t in range(SLOTS):
                 for g in range(2):
                     nc.tensor.matmul_mx(
                         out=bank[:, t, :],
-                        lhsT=codes[:, g, t, P * c_at : P * (c_at + 1)].bitcast(FP8X4),
-                        lhsT_scale=scl[:, g, t, 32 * s_at : 32 * (s_at + 1)].bitcast(U8),
-                        rhs=w_codes[:, g, c0 // 2 : c0 // 2 + 64].bitcast(U8).bitcast(FP4X4),
-                        rhs_scale=w_scl[:, g, c0 // 4 : c0 // 4 + 32].bitcast(U8),
+                        lhsT=codes[:, g, t, codes_at : codes_at + P].bitcast(FP8X4),
+                        lhsT_scale=plane[:, g, t, plane_at : plane_at + P // 4].bitcast(U8),
+                        rhs=w_codes[:, g, c0 // 2 : (c0 + P) // 2].bitcast(U8).bitcast(FP4X4),
+                        rhs_scale=w_plane[:, g, c0 // 4 : (c0 + P) // 4].bitcast(U8),
                         start=(g == 0),
                         stop=(g == 1),
                     )
-
-        def tanh(grp, b):
             if b == 0:
-                t_tile[grp] = work.tile([P, 512, 4], F32, name="tanh_z", align_bytes=64)
+                tanh_tiles[block] = work.tile([P, K_PASS, SLOTS], F32, name="tanh_z", align_bytes=ALIGN)
             nc.scalar.activation(
-                out=t_tile[grp][:, P * b : P * (b + 1), :],
-                in_=z_bank[grp, b][:].rearrange("p t n -> p n t"),
-                func=ACT.Tanh,
+                out=tanh_tiles[block][:, P * b : P * (b + 1), :], in_=bank[:].rearrange("p t n -> p n t"), func=ACT.Tanh
             )
 
-        def wmul(grp, b0, b1):
-            if b0 == 0:
-                h_tile[grp] = work.tile([P, 512, 4], BF16, name="h_bf", align_bytes=64)
+        def weigh(block, b0, b1, staged, weights):
+            h_tiles[block, b0] = staged[:, : P * (b1 - b0), :]
             nc.vector.tensor_tensor(
-                out=h_tile[grp][:, P * b0 : P * b1, :],
-                in0=t_tile[grp][:, P * b0 : P * b1, :],
-                in1=sw[:, grp % 4, :].unsqueeze(1).to_broadcast([P, P * (b1 - b0), 4]),
+                out=h_tiles[block, b0],
+                in0=tanh_tiles[block][:, P * b0 : P * b1, :],
+                in1=weights[:, :, block % GROUPS].unsqueeze(1).to_broadcast([P, P * (b1 - b0), SLOTS]),
                 op=ALU.mult,
             )
 
-        def qh(grp, b0, b1):
-            cols = slice(512 * (grp // 4) + P * b0, 512 * (grp // 4) + P * b1)
+        def h_staging():
+            return work.tile([P, K_PASS, SLOTS], BF16, name="h_bf", align_bytes=ALIGN)
+
+        def gpsimd_staging():
+            return work.tile([P, 2 * P, SLOTS], BF16, name="gpsimd_bf", bufs=1, align_bytes=ALIGN)
+
+        def quantise_h(block, b0, b1):
+            c0 = K_PASS * (block // GROUPS)
+            cols = slice(c0 + P * b0, c0 + P * b1)
             nc.vector.quantize_mx(
-                out=h_codes[:, grp % 4, cols].bitcast(FP8X4),
-                scales=h_scl[:, grp % 4, cols],
-                in_=h_tile[grp][:, P * b0 : P * b1, :].rearrange("p n t -> p (n t)"),
+                out=h_codes[:, block % GROUPS, cols].bitcast(FP8X4),
+                scales=h_plane[:, block % GROUPS, cols],
+                in_=h_tiles[block, b0].rearrange("p n t -> p (n t)"),
             )
 
-        def rint(ft, s0, s1, copy):
-            if ft not in r_tile:
-                r_tile[ft] = work.tile([P, NSG, P, 4], BF16, name="r_bf", align_bytes=64, bufs=RB)
-            copy(
-                out=r_tile[ft][:, s0:s1].rearrange("p s (c i) t -> p s c t i", i=4),
+        def interleave_r_scalar(ft, s0, s1):
+            if ft not in r_tiles:
+                r_tiles[ft] = work.tile([P, GROUPS, P, SLOTS], BF16, name="r_bf", bufs=4, align_bytes=ALIGN)
+            nc.scalar.copy(
+                out=r_tiles[ft][:, s0:s1].rearrange("p s (c i) t -> p s c t i", i=4),
                 in_=r_raw[:, s0:s1, :, P * ft : P * (ft + 1)].rearrange("p s t (c i) -> p s c t i", i=4),
             )
 
-        def qr(ft):
+        def interleave_r_gpsimd(ft, s0):
+            r_halves[ft, s0] = gpsimd_staging()[:].rearrange("p (s f) t -> p s f t", s=2)
+            gpsimd_copy(r_halves[ft, s0], r_raw[:, s0 : s0 + 2, :, P * ft : P * (ft + 1)].rearrange("p s t f -> p s f t"))
+
+        def quantise_r(ft, s0, s1):
+            staged = r_halves[ft, s0] if (ft, s0) in r_halves else r_tiles[ft][:, s0:s1]
             nc.vector.quantize_mx(
-                out=r_codes[:, ft].rearrange("p s f -> p (s f)").bitcast(FP8X4),
-                scales=r_scl[:, ft].rearrange("p s f -> p (s f)"),
-                in_=r_tile[ft][:].rearrange("p s f t -> p (s f t)"),
+                out=r_codes[:, ft, s0:s1].rearrange("p s f -> p (s f)").bitcast(FP8X4),
+                scales=r_plane[:, ft, s0:s1].rearrange("p s f -> p (s f)"),
+                in_=staged.rearrange("p s f t -> p (s f t)"),
             )
 
-        def mm2(ft, ch):
-            bank = psum.tile([P, 512], F32, name="bank%d" % (3 + (count["acc"] + 2) % 5))
-            count["acc"] += 1
-            acc_bank[ft, ch] = bank
-            for sg in range(NSG):
+        def moment(ft, half, s0=0, s1=GROUPS):
+            if s0 == 0:
+                y_banks[ft, half] = bank_tile([P, K_PASS], Y_BANKS[len(y_banks)])
+            cols = slice(K_PASS * half, K_PASS * (half + 1))
+            for group in range(s0, s1):
                 nc.tensor.matmul_mx(
-                    out=bank[:],
-                    lhsT=r_codes[:, ft, sg, :].bitcast(FP8X4),
-                    lhsT_scale=r_scl[:, ft, sg, :],
-                    rhs=h_codes[:, sg, 512 * ch : 512 * (ch + 1)].bitcast(FP8X4),
-                    rhs_scale=h_scl[:, sg, 512 * ch : 512 * (ch + 1)],
-                    start=(sg == 0),
-                    stop=(sg == NSG - 1),
+                    out=y_banks[ft, half][:],
+                    lhsT=r_codes[:, ft, group, :].bitcast(FP8X4),
+                    lhsT_scale=r_plane[:, ft, group, :],
+                    rhs=h_codes[:, group, cols].bitcast(FP8X4),
+                    rhs_scale=h_plane[:, group, cols],
+                    start=(group == 0),
+                    stop=(group == GROUPS - 1),
                 )
 
-        def scale_out(ft, ch):
-            j, i = 2 * (ft // 2) + ch, ft % 2
+        def scaled(out, sums, gains):
+            nc.vector.scalar_tensor_tensor(out=out, in0=sums, scalar=1.0 / S, in1=gains, op0=ALU.mult, op1=ALU.mult)
+
+        def scale_tile(ft, half):
+            fp, i = divmod(ft, 2)
             if i == 0:
-                y_tile[j] = work.tile([P, 2, 512], F32, name="y", bufs=4, align_bytes=64)
-            cols = slice(512 * ch, 512 * (ch + 1))
-            nc.vector.scalar_tensor_tensor(
-                out=y_tile[j][:, i, :], in0=acc_bank[ft, ch][:], scalar=1.0 / S, in1=gain_all[:, cols],
-                op0=ALU.mult, op1=ALU.mult,
+                y_tiles[fp, half] = work.tile([P, 2, K_PASS], F32, name="y", bufs=4, align_bytes=ALIGN)
+            scaled(y_tiles[fp, half][:, i, :], y_banks[ft, half][:], gain_rows[:, K_PASS * half : K_PASS * (half + 1)])
+
+        def store_y(fp, half, i0=0, i1=2):
+            rows = out_0[P * (2 * fp + i0) : P * (2 * fp + i1), K_PASS * half : K_PASS * (half + 1)]
+            nc.sync.dma_start(out=rows.rearrange("(i p) c -> p i c", p=P), in_=y_tiles[fp, half][:, i0:i1])
+
+        def scale_pair(fp, half):
+            scale_tile(2 * fp, half)
+            scale_tile(2 * fp + 1, half)
+            store_y(fp, half)
+
+        def by_word(ap):
+            return ap.rearrange("p (q u e) -> p u q e", u=2, e=2)
+
+        def y_bf(fp, half):
+            if (fp, half) not in y_bf_tiles:
+                y_bf_tiles[fp, half] = work.tile([P, 2, 2, P, 2], BF16, name="y_bf", bufs=4, align_bytes=ALIGN)
+            return y_bf_tiles[fp, half]
+
+        def round_pair_scalar(fp, half):
+            nc.scalar.copy(
+                out=y_bf(fp, half)[:], in_=y_tiles[fp, half][:].rearrange("p i (q u e) -> p i u q e", u=2, e=2)
             )
-            if j == 7:
-                nc.sync.dma_start(out=out_0[P * ft : P * (ft + 1), cols], in_=y_tile[j][:, i, :])
-            elif i == 1:
-                nc.sync.dma_start(
-                    out=out_0[P * (ft - 1) : P * (ft + 1), cols].rearrange("(i p) c -> p i c", i=2), in_=y_tile[j][:]
-                )
 
-        def yb_of(j):
-            if j not in yb_tile:
-                yb_tile[j] = work.tile([P, 2, 2, P, 2], BF16, name="y_bf", bufs=4, align_bytes=64)
-            return yb_tile[j]
-
-        def cast(j, i0, i1, copy):
-            copy(out=yb_of(j)[:, i0:i1], in_=y_tile[j][:, i0:i1].rearrange("p i (q u e) -> p i u q e", u=2, e=2))
-
-        def cast_direct(j, i0, i1):
-            ft, ch = 2 * (j // 2) + i0, j % 2
-            acc = acc_bank[ft, ch][:].rearrange("p (q u e) -> p u q e", u=2, e=2)
-            gv = gain_all[:, 512 * ch : 512 * (ch + 1)].rearrange("p (q u e) -> p u q e", u=2, e=2)
-            for u in range(2):
-                nc.vector.scalar_tensor_tensor(
-                    out=yb_of(j)[:, i0, u], in0=acc[:, u], scalar=1.0 / S, in1=gv[:, u], op0=ALU.mult, op1=ALU.mult
-                )
-
-        def tr(j, i0, i1):
-            bank = psum.tile([P, 2, 2, P], F32, name="bank%d" % (count["tr"] % 3))
-            count["tr"] += 1
-            tr_bank[j, i0] = bank
-            words = yb_tile[j][:].rearrange("p i u q e -> p i u (q e)").bitcast(F32)
+        def turn(fp, half, i0=0, i1=2):
+            bank = bank_tile([P, 2, 2, P], len(turned) % TURN_BANKS)
+            turned[fp, half, i0] = bank
+            words = y_bf_tiles[fp, half][:].rearrange("p i u q e -> p i u (q e)").bitcast(F32)
             for i in range(i0, i1):
                 for u in range(2):
-                    nc.tensor.transpose(bank[:, i, u, :], words[:, i, u, :], ident[:])
+                    nc.tensor.transpose(bank[:, i, u, :], words[:, i, u, :], identity[:])
+            y_words = work.tile([P, 2, P, 2], F32, name="y_words", bufs=4, align_bytes=ALIGN)
+            y_word_tiles[fp, half, i0] = y_words
+            nc.scalar.copy(out=y_words[:, i0:i1], in_=bank[:, i0:i1].rearrange("p i u f -> p i f u"))
 
-        def trcopy(j, i0, i1, copy):
-            yw = work.tile([P, 2, P, 2], F32, name="y_words", bufs=4, align_bytes=64)
-            yw_tile[j, i0] = yw
-            copy(out=yw[:, i0:i1], in_=tr_bank[j, i0][:, i0:i1].rearrange("p i u f -> p i f u"))
-
-        def qy(j, i0, i1):
-            f0, ch = 2 * P * (j // 2), j % 2
-            cols = slice(f0 + P * i0, f0 + P * i1)
+        def quantise_y(fp, half, i0=0, i1=2):
             nc.vector.quantize_mx(
-                out=y_codes[:, j // 2, ch, P * i0 : P * i1].bitcast(FP8X4),
-                scales=y_scl[:, ch, cols],
-                in_=yw_tile[j, i0][:, i0:i1].rearrange("p i f u -> p (i f u)").bitcast(BF16),
+                out=y_codes[:, fp, half, P * i0 : P * i1].bitcast(FP8X4),
+                scales=y_plane[:, half, P * (2 * fp + i0) : P * (2 * fp + i1)],
+                in_=y_word_tiles[fp, half, i0][:, i0:i1].rearrange("p i f u -> p (i f u)").bitcast(BF16),
             )
-            pair = slice(f0, f0 + 2 * P)
-            if j >= 6 and i1 == 2:
-                nc.sync.dma_start(out=o1[:, ch, pair], in_=y_codes[:, j // 2, ch])
-            elif j < 6 and ch == 1:
-                nc.sync.dma_start(out=o1[:, :, pair], in_=y_codes[:, j // 2])
-            if j == 7 and i1 == 2:
-                for q in range(4):
-                    eng = nc.sync if q % 2 == 0 else nc.scalar
-                    eng.dma_start(out=o2[4 * q : 4 * q + 4], in_=y_scl[32 * q : 32 * q + 4].bitcast(I32))
 
-        steps = {
-            "swperm": swperm, "swturn": swturn, "xperm": xperm, "xsperm": xsperm, "mm1": mm1, "tanh": tanh,
-            "wmul": wmul, "qh": qh,
-            "rintA": lambda *a: rint(*a, nc.scalar.copy),
-            "rintV": lambda *a: rint(*a, nc.vector.tensor_copy),
-            "qr": qr, "mm2": mm2, "gain": scale_out,
-            "cast": lambda *a: cast(*a, nc.scalar.copy),
-            "castV": lambda *a: cast(*a, nc.vector.tensor_copy),
-            "castD": cast_direct, "tr": tr,
-            "trcopy": lambda *a: trcopy(*a, nc.scalar.copy),
-            "trcopyV": lambda *a: trcopy(*a, nc.vector.tensor_copy),
-            "qy": qy,
-        }
-        for step in PLAN:
-            steps[step[0]](*step[1:])
+        def store_codes(fp, h0=0, h1=2):
+            nc.sync.dma_start(out=out_words_i[:, h0:h1, 2 * P * fp : 2 * P * (fp + 1)], in_=y_codes[:, fp, h0:h1])
+
+        reorder_x(0)
+        reorder_x_scales(0)
+        tanh_quarter(0, 0)
+        reorder_x_scales(1)
+        reorder_weights()
+        reorder_x(1)
+        reorder_x(2)
+        tanh_quarter(0, 1)
+        weights = turn_weights()
+        weigh(0, 0, 2, h_staging(), weights)
+        tanh_quarter(0, 2)
+        tanh_quarter(0, 3)
+        weigh(0, 2, 4, h_staging(), weights)
+        quantise_h(0, 0, 2)
+        tanh_quarter(1, 0)
+        tanh_quarter(1, 1)
+        weigh(1, 0, 2, gpsimd_staging(), weights)
+        quantise_h(0, 2, 4)
+        tanh_quarter(1, 2)
+        tanh_quarter(1, 3)
+        weigh(1, 2, 4, h_staging(), weights)
+        quantise_h(1, 0, 2)
+        waiting = (1, 2, 4)
+        for block in range(2, 2 * GROUPS):
+            for b in range(4):
+                tanh_quarter(block, b)
+            if block in SCALAR_HALVES:
+                ft, s0 = SCALAR_HALVES[block]
+                interleave_r_scalar(ft, s0, s0 + 2)
+            ft, s0 = GPSIMD_HALVES[block]
+            interleave_r_gpsimd(ft, s0)
+            weigh(block, 0, 4, h_staging(), weights)
+            quantise_h(*waiting)
+            waiting = (block, 0, 4)
+            quantise_r(ft, s0, s0 + 2)
+            if block in SCALAR_HALVES_QUANTISED:
+                quantise_r(*SCALAR_HALVES_QUANTISED[block])
+        quantise_h(*waiting)
+
+        for ft in range(4):
+            moment(ft, 0)
+        for s0, s1 in ((0, 2), (2, 3), (3, 4)):
+            for ft in range(4):
+                moment(ft, 1, s0, s1)
+
+        interleave_r_scalar(4, 2, 4)
+        quantise_r(4, 2, 4)
+        interleave_r_scalar(5, 0, 4)
+        scale_pair(0, 0)
+        for i in range(2):
+            gpsimd_copy(y_bf(0, 0)[:, i], by_word(y_tiles[0, 0][:, i]))
+        quantise_r(5, 0, 4)
+        interleave_r_scalar(6, 0, 4)
+        interleave_r_scalar(7, 0, 4)
+        scale_pair(1, 0)
+        round_pair_scalar(1, 0)
+        moment(4, 0)
+        moment(5, 0)
+        for fp in range(2):
+            scale_pair(fp, 1)
+            round_pair_scalar(fp, 1)
+        moment(4, 1)
+        turn(0, 0)
+        turn(1, 0)
+        quantise_r(6, 0, 4)
+        moment(5, 1)
+        scale_pair(2, 0)
+        round_pair_scalar(2, 0)
+        moment(6, 0)
+        turn(0, 1)
+        turn(1, 1)
+        quantise_r(7, 0, 4)
+        moment(7, 0)
+        scale_pair(2, 1)
+        round_pair_scalar(2, 1)
+        quantise_y(0, 0)
+        quantise_y(1, 0)
+        moment(6, 1)
+        moment(7, 1)
+        scale_pair(3, 0)
+        round_pair_scalar(3, 0)
+        for fp in range(2):
+            quantise_y(fp, 1)
+            store_codes(fp)
+
+        scale_tile(6, 1)
+        store_y(3, 1, 0, 1)
+        nc.vector.tensor_copy(out=y_bf(3, 1)[:, 0], in_=by_word(y_tiles[3, 1][:, 0]))
+        for u in range(2):
+            scaled(y_bf(3, 1)[:, 1, u], by_word(y_banks[7, 1][:])[:, u], by_word(gain_rows[:, K_PASS:C])[:, u])
+        scale_tile(7, 1)
+        store_y(3, 1, 1, 2)
+        for half in range(2):
+            turn(2, half)
+            quantise_y(2, half)
+        store_codes(2)
+        turn(3, 0)
+        quantise_y(3, 0)
+        store_codes(3, 0, 1)
+        for i in range(2):
+            turn(3, 1, i, i + 1)
+        for i in range(2):
+            quantise_y(3, 1, i, i + 1)
+        store_codes(3, 1, 2)
+        for q, (live, rows) in enumerate(quadrants):
+            queue = nc.sync if q % 2 == 0 else nc.scalar
+            queue.dma_start(out=out_scales_i[rows], in_=y_plane[live].bitcast(I32))

from contextlib import ExitStack

import concourse.mybir as mybir
from concourse.masks import make_identity

S, F, C = 2048, 1024, 1024
FLOPS = 2 * S * F * C * 2

F32 = mybir.dt.float32
BF16 = mybir.dt.bfloat16
I32 = mybir.dt.int32
U8 = mybir.dt.uint8
FP8X4 = mybir.dt.float8_e4m3fn_x4
FP4X4 = mybir.dt.float4_e2m1fn_x4
ACT = mybir.ActivationFunctionType
ALU = mybir.AluOpType

P = 128
SLOTS = 4
K_PASS = P * SLOTS
GROUPS = S // K_PASS
F_TILES = F // P
ALIGN = 64

Z_BANKS = 4
WEIGHT_BANK = 7
Y_BANKS = [4, 5, 6, 0, 1, 2, 3, 7, 4, 5, 6, 3, 7, 4, 5, 6]
TURN_BANKS = 3

GPSIMD_HALVES = {2: (0, 0), 3: (1, 0), 4: (0, 2), 5: (1, 2), 6: (3, 0), 7: (4, 0)}
SCALAR_HALVES = {4: (2, 0), 5: (2, 2), 6: (3, 2)}
SCALAR_HALVES_QUANTISED = {5: (2, 0, 4), 6: (3, 2, 4)}


def tile_tanh_cross_moment_planes_h2_kernel(
    tc, x_words, x_scales, w_words, w_scales, x_rows, sample_weight, gain, out_0, out_1, out_2
):
    nc = tc.nc
    with ExitStack() as ctx:
        keep = ctx.enter_context(tc.tile_pool(name="keep", bufs=1))
        work = ctx.enter_context(tc.tile_pool(name="work", bufs=3))
        psum = ctx.enter_context(tc.psum_pool(name="psum", bufs=1))
        ctx.enter_context(tc.manual_schedule())

        x_parts, scale_parts = (1, 1, 2), (1, 3)
        x_raw = [keep.tile([P, 2, K_PASS * n], I32, name="x_raw%d" % i, align_bytes=ALIGN) for i, n in enumerate(x_parts)]
        x_codes = [keep.tile([P, 2, SLOTS, P * n], I32, name="x_codes%d" % i, align_bytes=ALIGN) for i, n in enumerate(x_parts)]
        x_scales_raw = keep.tile([P, 2, S // 4], I32, align_bytes=ALIGN)
        x_planes = [keep.tile([P, 2, SLOTS, P // 4 * n], I32, name="x_plane%d" % i, align_bytes=ALIGN) for i, n in enumerate(scale_parts)]
        w_codes = keep.tile([P, 2, C // 2], I32, align_bytes=ALIGN)
        w_plane = keep.tile([P, 2, C // 4], I32, align_bytes=ALIGN)
        r_raw = keep.tile([P, GROUPS, SLOTS, F], BF16, align_bytes=ALIGN)
        weight_raw = keep.tile([GROUPS, K_PASS], BF16, align_bytes=ALIGN)
        weight_rows = keep.tile([P, SLOTS, P], F32, align_bytes=ALIGN)
        zero = keep.tile([P, 1], F32, align_bytes=ALIGN)
        gain_rows = keep.tile([P, C], BF16, align_bytes=ALIGN)
        identity = keep.tile([P, P], F32, align_bytes=ALIGN)
        h_codes = keep.tile([P, GROUPS, C], I32, align_bytes=ALIGN)
        h_plane = keep.tile([P, GROUPS, C], U8, align_bytes=ALIGN)
        r_codes = keep.tile([P, F_TILES, GROUPS, P], I32, align_bytes=ALIGN)
        r_plane = keep.tile([P, F_TILES, GROUPS, P], U8, align_bytes=ALIGN)
        y_codes = keep.tile([P, F_TILES // 2, 2, 2 * P], I32, align_bytes=ALIGN)
        y_plane = keep.tile([P, 2, F], U8, align_bytes=ALIGN)

        x_words_i = x_words.rearrange("g p n t -> p g (n t)").bitcast(I32)
        w_words_i = w_words.rearrange("g p b -> p g b").bitcast(I32)
        x_scales_i = x_scales.rearrange("g q n -> q g n").bitcast(I32)
        w_scales_i = w_scales.rearrange("g q n -> q g n").bitcast(I32)
        out_words_i = out_1.rearrange("g p m t -> p g (m t)").bitcast(I32)
        out_scales_i = out_2.rearrange("g q n -> q g n").bitcast(I32)
        quadrants = [(slice(32 * q, 32 * q + 4), slice(4 * q, 4 * q + 4)) for q in range(4)]

        for live, rows in quadrants:
            nc.sync.dma_start(out=x_scales_raw[live], in_=x_scales_i[rows])
        nc.scalar.dma_start(out=x_raw[0][:], in_=x_words_i[:, :, 0:K_PASS])
        nc.scalar.dma_start(out=w_codes[:], in_=w_words_i)
        nc.vector.memset(w_plane[:], 0)
        nc.vector.memset(zero[:], 0.0)
        for plane in x_planes:
            nc.vector.memset(plane[:], 0)
        for live, rows in quadrants:
            nc.sync.dma_start(out=w_plane[live], in_=w_scales_i[rows])
        nc.scalar.activation(
            out=weight_rows[:].rearrange("p t m -> p (t m)"), in_=zero[:].to_broadcast([P, SLOTS * P]), func=ACT.Tanh
        )
        nc.sync.dma_start(out=weight_raw[:], in_=sample_weight.rearrange("(s n) -> s n", s=GROUPS))
        nc.sync.dma_start(out=x_raw[1][:], in_=x_words_i[:, :, K_PASS : 2 * K_PASS])
        nc.sync.dma_start(out=x_raw[2][:], in_=x_words_i[:, :, 2 * K_PASS : S])
        for group in range(GROUPS):
            rows = x_rows[K_PASS * group : K_PASS * (group + 1), :].rearrange("(j t r) f -> r j t f", t=SLOTS, r=4)
            for r in range(4):
                nc.sync.dma_start(out=r_raw[r:P:4, group], in_=rows[r])
        nc.sync.dma_start(out=gain_rows[:], in_=gain.partition_broadcast(P))
        make_identity(nc, identity[:])

        tanh_tiles, h_tiles, r_tiles, r_halves = {}, {}, {}, {}
        y_banks, y_tiles, y_bf_tiles, turned, y_word_tiles = {}, {}, {}, {}, {}

        def bank_tile(shape, bank):
            return psum.tile(shape, F32, name="bank%d" % bank)

        def gpsimd_copy(out, in_):
            nc.gpsimd.tensor_scalar(out=out, in0=in_, scalar1=1.0, scalar2=0.0, op0=ALU.mult, op1=ALU.add)

        def reorder_x(part):
            nc.vector.tensor_copy(
                out=x_codes[part][:].rearrange("p g t (j r) -> p g t j r", r=4),
                in_=x_raw[part][:].rearrange("p g (j t r) -> p g t j r", t=SLOTS, r=4),
            )

        def reorder_x_scales(part):
            lo = P * sum(scale_parts[:part])
            for live, rows in quadrants:
                nc.vector.tensor_copy(
                    out=x_planes[part][live],
                    in_=x_scales_raw[live, :, lo : lo + P * scale_parts[part]].rearrange("p g (j t) -> p g t j", t=SLOTS),
                )

        def reorder_weights():
            nc.vector.tensor_copy(
                out=weight_rows[0:GROUPS].rearrange("s t (j r) -> s t j r", r=4),
                in_=weight_raw[:].rearrange("s (j t r) -> s t j r", t=SLOTS, r=4),
            )

        def turn_weights():
            bank = bank_tile([P, SLOTS, P], WEIGHT_BANK)
            for t in range(SLOTS):
                nc.tensor.transpose(bank[:, t, :], weight_rows[:, t, :], identity[:])
            return bank

        def tanh_quarter(block, b):
            group, c0 = block % GROUPS, K_PASS * (block // GROUPS) + P * b
            codes, codes_at = x_codes[min(group, 2)], P * max(group - 2, 0)
            plane, plane_at = x_planes[min(group, 1)], P // 4 * max(group - 1, 0)
            bank = bank_tile([P, SLOTS, P], (4 * block + b) % Z_BANKS)
            for t in range(SLOTS):
                for g in range(2):
                    nc.tensor.matmul_mx(
                        out=bank[:, t, :],
                        lhsT=codes[:, g, t, codes_at : codes_at + P].bitcast(FP8X4),
                        lhsT_scale=plane[:, g, t, plane_at : plane_at + P // 4].bitcast(U8),
                        rhs=w_codes[:, g, c0 // 2 : (c0 + P) // 2].bitcast(U8).bitcast(FP4X4),
                        rhs_scale=w_plane[:, g, c0 // 4 : (c0 + P) // 4].bitcast(U8),
                        start=(g == 0),
                        stop=(g == 1),
                    )
            if b == 0:
                tanh_tiles[block] = work.tile([P, K_PASS, SLOTS], F32, name="tanh_z", align_bytes=ALIGN)
            nc.scalar.activation(
                out=tanh_tiles[block][:, P * b : P * (b + 1), :], in_=bank[:].rearrange("p t n -> p n t"), func=ACT.Tanh
            )

        def weigh(block, b0, b1, staged, weights):
            h_tiles[block, b0] = staged[:, : P * (b1 - b0), :]
            nc.vector.tensor_tensor(
                out=h_tiles[block, b0],
                in0=tanh_tiles[block][:, P * b0 : P * b1, :],
                in1=weights[:, :, block % GROUPS].unsqueeze(1).to_broadcast([P, P * (b1 - b0), SLOTS]),
                op=ALU.mult,
            )

        def h_staging():
            return work.tile([P, K_PASS, SLOTS], BF16, name="h_bf", align_bytes=ALIGN)

        def gpsimd_staging():
            return work.tile([P, 2 * P, SLOTS], BF16, name="gpsimd_bf", bufs=1, align_bytes=ALIGN)

        def quantise_h(block, b0, b1):
            c0 = K_PASS * (block // GROUPS)
            cols = slice(c0 + P * b0, c0 + P * b1)
            nc.vector.quantize_mx(
                out=h_codes[:, block % GROUPS, cols].bitcast(FP8X4),
                scales=h_plane[:, block % GROUPS, cols],
                in_=h_tiles[block, b0].rearrange("p n t -> p (n t)"),
            )

        def interleave_r_scalar(ft, s0, s1):
            if ft not in r_tiles:
                r_tiles[ft] = work.tile([P, GROUPS, P, SLOTS], BF16, name="r_bf", bufs=4, align_bytes=ALIGN)
            nc.scalar.copy(
                out=r_tiles[ft][:, s0:s1].rearrange("p s (c i) t -> p s c t i", i=4),
                in_=r_raw[:, s0:s1, :, P * ft : P * (ft + 1)].rearrange("p s t (c i) -> p s c t i", i=4),
            )

        def interleave_r_gpsimd(ft, s0):
            r_halves[ft, s0] = gpsimd_staging()[:].rearrange("p (s f) t -> p s f t", s=2)
            gpsimd_copy(r_halves[ft, s0], r_raw[:, s0 : s0 + 2, :, P * ft : P * (ft + 1)].rearrange("p s t f -> p s f t"))

        def quantise_r(ft, s0, s1):
            staged = r_halves[ft, s0] if (ft, s0) in r_halves else r_tiles[ft][:, s0:s1]
            nc.vector.quantize_mx(
                out=r_codes[:, ft, s0:s1].rearrange("p s f -> p (s f)").bitcast(FP8X4),
                scales=r_plane[:, ft, s0:s1].rearrange("p s f -> p (s f)"),
                in_=staged.rearrange("p s f t -> p (s f t)"),
            )

        def moment(ft, half, s0=0, s1=GROUPS):
            if s0 == 0:
                y_banks[ft, half] = bank_tile([P, K_PASS], Y_BANKS[len(y_banks)])
            cols = slice(K_PASS * half, K_PASS * (half + 1))
            for group in range(s0, s1):
                nc.tensor.matmul_mx(
                    out=y_banks[ft, half][:],
                    lhsT=r_codes[:, ft, group, :].bitcast(FP8X4),
                    lhsT_scale=r_plane[:, ft, group, :],
                    rhs=h_codes[:, group, cols].bitcast(FP8X4),
                    rhs_scale=h_plane[:, group, cols],
                    start=(group == 0),
                    stop=(group == GROUPS - 1),
                )

        def scaled(out, sums, gains):
            nc.vector.scalar_tensor_tensor(out=out, in0=sums, scalar=1.0 / S, in1=gains, op0=ALU.mult, op1=ALU.mult)

        def scale_tile(ft, half):
            fp, i = divmod(ft, 2)
            if i == 0:
                y_tiles[fp, half] = work.tile([P, 2, K_PASS], F32, name="y", bufs=4, align_bytes=ALIGN)
            scaled(y_tiles[fp, half][:, i, :], y_banks[ft, half][:], gain_rows[:, K_PASS * half : K_PASS * (half + 1)])

        def store_y(fp, half, i0=0, i1=2):
            rows = out_0[P * (2 * fp + i0) : P * (2 * fp + i1), K_PASS * half : K_PASS * (half + 1)]
            nc.sync.dma_start(out=rows.rearrange("(i p) c -> p i c", p=P), in_=y_tiles[fp, half][:, i0:i1])

        def scale_pair(fp, half):
            scale_tile(2 * fp, half)
            scale_tile(2 * fp + 1, half)
            store_y(fp, half)

        def by_word(ap):
            return ap.rearrange("p (q u e) -> p u q e", u=2, e=2)

        def y_bf(fp, half):
            if (fp, half) not in y_bf_tiles:
                y_bf_tiles[fp, half] = work.tile([P, 2, 2, P, 2], BF16, name="y_bf", bufs=4, align_bytes=ALIGN)
            return y_bf_tiles[fp, half]

        def round_pair_scalar(fp, half):
            nc.scalar.copy(
                out=y_bf(fp, half)[:], in_=y_tiles[fp, half][:].rearrange("p i (q u e) -> p i u q e", u=2, e=2)
            )

        def turn(fp, half, i0=0, i1=2):
            bank = bank_tile([P, 2, 2, P], len(turned) % TURN_BANKS)
            turned[fp, half, i0] = bank
            words = y_bf_tiles[fp, half][:].rearrange("p i u q e -> p i u (q e)").bitcast(F32)
            for i in range(i0, i1):
                for u in range(2):
                    nc.tensor.transpose(bank[:, i, u, :], words[:, i, u, :], identity[:])
            y_words = work.tile([P, 2, P, 2], F32, name="y_words", bufs=4, align_bytes=ALIGN)
            y_word_tiles[fp, half, i0] = y_words
            nc.scalar.copy(out=y_words[:, i0:i1], in_=bank[:, i0:i1].rearrange("p i u f -> p i f u"))

        def quantise_y(fp, half, i0=0, i1=2):
            nc.vector.quantize_mx(
                out=y_codes[:, fp, half, P * i0 : P * i1].bitcast(FP8X4),
                scales=y_plane[:, half, P * (2 * fp + i0) : P * (2 * fp + i1)],
                in_=y_word_tiles[fp, half, i0][:, i0:i1].rearrange("p i f u -> p (i f u)").bitcast(BF16),
            )

        def store_codes(fp, h0=0, h1=2):
            nc.sync.dma_start(out=out_words_i[:, h0:h1, 2 * P * fp : 2 * P * (fp + 1)], in_=y_codes[:, fp, h0:h1])

        reorder_x(0)
        reorder_x_scales(0)
        tanh_quarter(0, 0)
        reorder_x_scales(1)
        reorder_weights()
        reorder_x(1)
        reorder_x(2)
        tanh_quarter(0, 1)
        weights = turn_weights()
        weigh(0, 0, 2, h_staging(), weights)
        tanh_quarter(0, 2)
        tanh_quarter(0, 3)
        weigh(0, 2, 4, h_staging(), weights)
        quantise_h(0, 0, 2)
        tanh_quarter(1, 0)
        tanh_quarter(1, 1)
        weigh(1, 0, 2, gpsimd_staging(), weights)
        quantise_h(0, 2, 4)
        tanh_quarter(1, 2)
        tanh_quarter(1, 3)
        weigh(1, 2, 4, h_staging(), weights)
        quantise_h(1, 0, 2)
        waiting = (1, 2, 4)
        for block in range(2, 2 * GROUPS):
            for b in range(4):
                tanh_quarter(block, b)
            if block in SCALAR_HALVES:
                ft, s0 = SCALAR_HALVES[block]
                interleave_r_scalar(ft, s0, s0 + 2)
            ft, s0 = GPSIMD_HALVES[block]
            interleave_r_gpsimd(ft, s0)
            weigh(block, 0, 4, h_staging(), weights)
            quantise_h(*waiting)
            waiting = (block, 0, 4)
            quantise_r(ft, s0, s0 + 2)
            if block in SCALAR_HALVES_QUANTISED:
                quantise_r(*SCALAR_HALVES_QUANTISED[block])
        quantise_h(*waiting)

        for ft in range(4):
            moment(ft, 0)
        for s0, s1 in ((0, 2), (2, 3), (3, 4)):
            for ft in range(4):
                moment(ft, 1, s0, s1)

        interleave_r_scalar(4, 2, 4)
        quantise_r(4, 2, 4)
        interleave_r_scalar(5, 0, 4)
        scale_pair(0, 0)
        for i in range(2):
            gpsimd_copy(y_bf(0, 0)[:, i], by_word(y_tiles[0, 0][:, i]))
        quantise_r(5, 0, 4)
        interleave_r_scalar(6, 0, 4)
        interleave_r_scalar(7, 0, 4)
        scale_pair(1, 0)
        round_pair_scalar(1, 0)
        moment(4, 0)
        moment(5, 0)
        for fp in range(2):
            scale_pair(fp, 1)
            round_pair_scalar(fp, 1)
        moment(4, 1)
        turn(0, 0)
        turn(1, 0)
        quantise_r(6, 0, 4)
        moment(5, 1)
        scale_pair(2, 0)
        round_pair_scalar(2, 0)
        moment(6, 0)
        turn(0, 1)
        turn(1, 1)
        quantise_r(7, 0, 4)
        moment(7, 0)
        scale_pair(2, 1)
        round_pair_scalar(2, 1)
        quantise_y(0, 0)
        quantise_y(1, 0)
        moment(6, 1)
        moment(7, 1)
        scale_pair(3, 0)
        round_pair_scalar(3, 0)
        for fp in range(2):
            quantise_y(fp, 1)
            store_codes(fp)

        scale_tile(6, 1)
        store_y(3, 1, 0, 1)
        nc.vector.tensor_copy(out=y_bf(3, 1)[:, 0], in_=by_word(y_tiles[3, 1][:, 0]))
        for u in range(2):
            scaled(y_bf(3, 1)[:, 1, u], by_word(y_banks[7, 1][:])[:, u], by_word(gain_rows[:, K_PASS:C])[:, u])
        scale_tile(7, 1)
        store_y(3, 1, 1, 2)
        for half in range(2):
            turn(2, half)
            quantise_y(2, half)
        store_codes(2)
        turn(3, 0)
        quantise_y(3, 0)
        store_codes(3, 0, 1)
        for i in range(2):
            turn(3, 1, i, i + 1)
        for i in range(2):
            quantise_y(3, 1, i, i + 1)
        store_codes(3, 1, 2)
        for q, (live, rows) in enumerate(quadrants):
            queue = nc.sync if q % 2 == 0 else nc.scalar
            queue.dma_start(out=out_scales_i[rows], in_=y_plane[live].bitcast(I32))
